import numpy as np
import ml_dtypes


def mxq(x, axis, fmt="e4m3"):
    dtype, down = {"e4m3": (ml_dtypes.float8_e4m3fn, 7), "e5m2": (ml_dtypes.float8_e5m2, 14)}[fmt]
    v = np.moveaxis(np.asarray(x, np.float32).astype(ml_dtypes.bfloat16).astype(np.float64), axis, -1)
    blocks = v.reshape(v.shape[:-1] + (-1, 32))
    amax = np.abs(blocks).max(-1, keepdims=True)
    byte = np.maximum(np.where(amax > 0, np.frexp(amax)[1] - 1 + 127, 0) - down, 1)
    scale = np.exp2(byte - 127.0)
    codes = (blocks / scale).astype(np.float32).astype(dtype).astype(np.float64)
    return np.moveaxis((codes * scale).reshape(v.shape), -1, axis)


WIDE = False


def mx_kscale(k):
    if not WIDE:
        return np.ones(k)
    levels = np.array([10, -10, 5, -5, 0])
    if k % 512:
        return np.exp2(np.random.permutation(np.resize(levels, k // 32))).repeat(32)
    a = np.empty((k // 512, 16))
    for p in range(k // 512):
        a[p, :8] = np.random.permutation(np.resize(levels, 8))
        for g in range(8):
            far = levels[np.abs(levels - a[p, g]) >= 10]
            a[p, g + 8] = far[np.random.randint(len(far))]
    return np.exp2(a.ravel()).repeat(32)


def f64(x):
    return np.asarray(x).astype(np.float64)


def striped(idx):
    return np.tile(idx.reshape(-1, 16).T, (8, 1)).astype(np.uint16)


def unstriped(offs):
    return offs[:16].T.reshape(-1).astype(np.int64)


def pack_weight(w):
    k, n = w.shape
    w = f64(np.asarray(w, np.float32).astype(ml_dtypes.bfloat16)).reshape(k // 32, 32, n)
    amax = np.abs(w).max(1)
    byte = np.clip(np.where(amax > 0, np.frexp(amax)[1] - 1 + 127 - 7, 1), 1, 254)
    scaled = (w * np.exp2(127.0 - byte)[:, None, :]).reshape(k, n).astype(np.float32)
    words = np.ascontiguousarray(scaled.reshape(k // 512, 128, 4, n).transpose(0, 1, 3, 2)).astype(ml_dtypes.float8_e4m3fn).view(np.uint8)
    return words, np.ascontiguousarray(byte.astype(np.uint8).reshape(k // 512, 16, n))


def unpack_weight(words, scales):
    g, p, n, _ = words.shape
    vals = np.ascontiguousarray(words).view(ml_dtypes.float8_e4m3fn).astype(np.float64) * np.repeat(np.exp2(scales.astype(np.float64) - 127.0), 8, axis=1)[..., None]
    return vals.transpose(0, 1, 3, 2).reshape(g * 512, n)


def relu(v):
    return np.maximum(v, 0.0)


K, T, S, N = 1024, 1024, 512, 128


def setup_inputs():
    n = np.random.standard_normal
    s = mx_kscale(K)[:, None]
    packed_xT = pack_weight(n((K, T)) * s)
    return {
        "x_words": packed_xT[0],
        "x_scales": packed_xT[1],
        "w1": (n((K, N)) / np.sqrt(2 * K) / s).astype(np.float32),
        "w2": (n((K, N)) / np.sqrt(2 * K) / s).astype(np.float32),
        "offs": striped(np.random.permutation(T)[:S]),
    }


def reference(x_words, x_scales, w1, w2, offs):
    xq = unpack_weight(x_words, x_scales)[:, unstriped(offs)]
    y0 = mxq(f64(w1), 0, "e4m3").T @ xq
    y1 = mxq(f64(w2), 0, "e4m3").T @ xq
    return relu(y0 + np.pad(y1, ((0, 0), (1, 0)))[:, :S])

@@ -1,0 +1,104 @@
+from contextlib import ExitStack
+
+import concourse.mybir as mybir
+
+K, T, S, N = 1024, 1024, 512, 128
+FLOPS = 2 * 2 * K * S * N
+
+F32 = mybir.dt.float32
+BF16 = mybir.dt.bfloat16
+I32 = mybir.dt.int32
+U32 = mybir.dt.uint32
+U16 = mybir.dt.uint16
+U8 = mybir.dt.uint8
+FP8X4 = mybir.dt.float8_e4m3fn_x4
+ACT = mybir.ActivationFunctionType
+
+P = 128
+PACK = 4
+K_PASS = P * PACK
+PASSES = K // K_PASS
+QUAD = 32
+SROWS = 4
+LEAD_W = 16
+LEAD_B = 64
+HALF = S // 2
+
+
+def tile_picked_listconv_relu_p_kernel(tc, x_words, x_scales, w1, w2, offs, out):
+    nc = tc.nc
+    with ExitStack() as ctx:
+        keep = ctx.enter_context(tc.tile_pool(name="keep", bufs=1))
+        psum = ctx.enter_context(tc.psum_pool(name="psum", bufs=1))
+
+        offsets = keep.tile([P, S // 16], U16, name="offsets")
+        nc.sync.dma_start(offsets[:], offs)
+
+        scale_table = keep.tile([P, T], U8, name="scale_table", align_bytes=64)
+        nc.vector.memset(scale_table[:].bitcast(I32), 0)
+        for q in range(P // QUAD):
+            nc.scalar.dma_start(
+                out=scale_table[QUAD * q : QUAD * q + PASSES * SROWS, :].bitcast(I32),
+                in_=x_scales[:, SROWS * q : SROWS * (q + 1), :].bitcast(I32),
+            )
+
+        weights = (w1, w2)
+        word_table = []
+        w_raw = {}
+        for g in range(PASSES):
+            table = keep.tile([P, T], I32, name="word_table%d" % g, align_bytes=64)
+            nc.sync.dma_start(out=table[:], in_=x_words[g].rearrange("p c r -> p (c r)").bitcast(I32))
+            word_table.append(table)
+            for d in range(2):
+                raw = keep.tile([P, PACK, N], F32, name="w_raw%d%d" % (d, g))
+                nc.sync.dma_start(out=raw[:], in_=weights[d][g * K_PASS : (g + 1) * K_PASS, :].rearrange("(p j) n -> p j n", j=PACK))
+                w_raw[d, g] = raw
+
+        picked_scales = keep.tile([P, LEAD_B + S], U8, name="picked_scales", align_bytes=64)
+        nc.vector.memset(picked_scales[:, :LEAD_B].bitcast(I32), 0)
+        picked_words = []
+        for g in range(PASSES):
+            picked = keep.tile([P, LEAD_W + S], I32, name="picked_words%d" % g, align_bytes=64)
+            nc.vector.memset(picked[:, :LEAD_W], 0)
+            picked_words.append(picked)
+
+        acc = [psum.tile([N, HALF], F32, name="acc%d" % h) for h in range(2)]
+
+        def product(d, g, words, planes):
+            grouped = keep.tile([P, N, PACK], BF16, name="grouped%d%d" % (d, g), align_bytes=64)
+            nc.scalar.activation(
+                grouped[:].rearrange("p (c i) t -> p c t i", i=4),
+                w_raw[d, g][:].rearrange("p t (c i) -> p c t i", i=4),
+                ACT.Copy,
+            )
+            codes = keep.tile([P, N], U32, name="codes%d%d" % (d, g), align_bytes=64)
+            scales = keep.tile([P, N], U8, name="scales%d%d" % (d, g), align_bytes=64)
+            nc.vector.quantize_mx(out=codes[:].bitcast(FP8X4), scales=scales[:], in_=grouped[:].rearrange("p n t -> p (n t)"))
+            for h in range(2):
+                nc.tensor.matmul_mx(
+                    out=acc[h][:],
+                    lhsT=codes[:].bitcast(FP8X4),
+                    lhsT_scale=scales[:],
+                    rhs=words[:, h * HALF : (h + 1) * HALF].bitcast(FP8X4),
+                    rhs_scale=planes[SROWS * g :, h * HALF : (h + 1) * HALF],
+                    start=(d == 0 and g == 0),
+                    stop=(d == 1 and g == PASSES - 1),
+                )
+
+        nc.vector.tensor_copy(picked_scales[:, LEAD_B:], scale_table[:].indirect(offsets[:]))
+        late_scales = keep.tile([P, S], U8, name="late_scales", align_bytes=64)
+        for g in range(PASSES):
+            nc.vector.tensor_copy(picked_words[g][:, LEAD_W:].bitcast(U32), word_table[g][:].bitcast(U32).indirect(offsets[:]))
+            product(0, g, picked_words[g][:, LEAD_W:], picked_scales[:, LEAD_B:])
+            if g == 0:
+                nc.vector.tensor_copy(late_scales[:], picked_scales[:, LEAD_B - 1 : LEAD_B - 1 + S])
+            late = keep.tile([P, S], I32, name="late_words%d" % g, align_bytes=64)
+            nc.vector.tensor_copy(late[:], picked_words[g][:, LEAD_W - 1 : LEAD_W - 1 + S])
+            product(1, g, late[:], late_scales[:])
+
+        result0 = keep.tile([N, HALF], F32, name="result0")
+        nc.vector.tensor_scalar_max(result0[:], acc[0][:], 0.0)
+        nc.sync.dma_start(out=out[:, :HALF], in_=result0[:])
+        result1 = keep.tile([N, HALF], F32, name="result1")
+        nc.scalar.activation(result1[:], acc[1][:], ACT.Relu)
+        nc.scalar.dma_start(out=out[:, HALF:], in_=result1[:])

@@ -28,13 +28,15 @@ HALF = S // 2
 def tile_picked_listconv_relu_p_kernel(tc, x_words, x_scales, w1, w2, offs, out):
     nc = tc.nc
     with ExitStack() as ctx:
+        lists = ctx.enter_context(tc.tile_pool(name="lists", bufs=1))
         keep = ctx.enter_context(tc.tile_pool(name="keep", bufs=1))
+        shared = ctx.enter_context(tc.tile_pool(name="shared", bufs=1))
         psum = ctx.enter_context(tc.psum_pool(name="psum", bufs=1))
 
-        offsets = keep.tile([P, S // 16], U16, name="offsets")
+        offsets = lists.tile([P, S // 16], U16, name="offsets")
         nc.sync.dma_start(offsets[:], offs)
 
-        scale_table = keep.tile([P, T], U8, name="scale_table", align_bytes=64)
+        scale_table = shared.tile([P, T], U8, name="scale_table", align_bytes=64, offset=4 * S - T // 2)
         nc.vector.memset(scale_table[:].bitcast(I32), 0)
         for q in range(P // QUAD):
             nc.scalar.dma_start(
@@ -42,38 +44,37 @@ def tile_picked_listconv_relu_p_kernel(tc, x_words, x_scales, w1, w2, offs, out)
                 in_=x_scales[:, SROWS * q : SROWS * (q + 1), :].bitcast(I32),
             )
 
-        weights = (w1, w2)
-        word_table = []
-        w_raw = {}
-        for g in range(PASSES):
-            table = keep.tile([P, T], I32, name="word_table%d" % g, align_bytes=64)
-            nc.sync.dma_start(out=table[:], in_=x_words[g].rearrange("p c r -> p (c r)").bitcast(I32))
-            word_table.append(table)
-            for d in range(2):
-                raw = keep.tile([P, PACK, N], F32, name="w_raw%d%d" % (d, g))
-                nc.sync.dma_start(out=raw[:], in_=weights[d][g * K_PASS : (g + 1) * K_PASS, :].rearrange("(p j) n -> p j n", j=PACK))
-                w_raw[d, g] = raw
+        table0 = keep.tile([P, T], I32, name="table0", tag="table0", align_bytes=64)
+        nc.sync.dma_start(out=table0[:], in_=x_words[0].rearrange("p c r -> p (c r)").bitcast(I32))
+        w1_raw = keep.tile([P, PASSES, PACK, N], F32, name="w1_raw")
+        nc.sync.dma_start(out=w1_raw[:], in_=w1.rearrange("(g p j) n -> p g j n", j=PACK, p=P))
+        w2_raw0 = keep.tile([P, PACK, N], F32, name="w2_raw0")
+        nc.sync.dma_start(out=w2_raw0[:], in_=w2[:K_PASS, :].rearrange("(p j) n -> p j n", j=PACK))
 
-        picked_scales = keep.tile([P, LEAD_B + S], U8, name="picked_scales", align_bytes=64)
-        nc.vector.memset(picked_scales[:, :LEAD_B].bitcast(I32), 0)
-        picked_words = []
+        late_scales = keep.tile([P, S], U8, name="late_scales", align_bytes=64)
+        nc.vector.memset(late_scales[:, :4].bitcast(I32), 0)
+        late_words = []
         for g in range(PASSES):
-            picked = keep.tile([P, LEAD_W + S], I32, name="picked_words%d" % g, align_bytes=64)
-            nc.vector.memset(picked[:, :LEAD_W], 0)
-            picked_words.append(picked)
+            late = keep.tile([P, S], I32, name="late_words%d" % g, align_bytes=64)
+            nc.vector.memset(late[:, :1], 0)
+            late_words.append(late)
 
         acc = [psum.tile([N, HALF], F32, name="acc%d" % h) for h in range(2)]
 
-        def product(d, g, words, planes):
-            grouped = keep.tile([P, N, PACK], BF16, name="grouped%d%d" % (d, g), align_bytes=64)
+        def quantize(raw, label):
+            grouped = keep.tile([P, N, PACK], BF16, name="grouped" + label, align_bytes=64)
             nc.scalar.activation(
                 grouped[:].rearrange("p (c i) t -> p c t i", i=4),
-                w_raw[d, g][:].rearrange("p t (c i) -> p c t i", i=4),
+                raw.rearrange("p t (c i) -> p c t i", i=4),
                 ACT.Copy,
             )
-            codes = keep.tile([P, N], U32, name="codes%d%d" % (d, g), align_bytes=64)
-            scales = keep.tile([P, N], U8, name="scales%d%d" % (d, g), align_bytes=64)
+            codes = keep.tile([P, N], U32, name="codes" + label, align_bytes=64)
+            scales = keep.tile([P, N], U8, name="scales" + label, align_bytes=64)
             nc.vector.quantize_mx(out=codes[:].bitcast(FP8X4), scales=scales[:], in_=grouped[:].rearrange("p n t -> p (n t)"))
+            return codes, scales
+
+        def product(stationary, words, planes, g, start, stop):
+            codes, scales = stationary
             for h in range(2):
                 nc.tensor.matmul_mx(
                     out=acc[h][:],
@@ -81,20 +82,32 @@ def tile_picked_listconv_relu_p_kernel(tc, x_words, x_scales, w1, w2, offs, out)
                     lhsT_scale=scales[:],
                     rhs=words[:, h * HALF : (h + 1) * HALF].bitcast(FP8X4),
                     rhs_scale=planes[SROWS * g :, h * HALF : (h + 1) * HALF],
-                    start=(d == 0 and g == 0),
-                    stop=(d == 1 and g == PASSES - 1),
+                    start=start,
+                    stop=stop,
                 )
 
-        nc.vector.tensor_copy(picked_scales[:, LEAD_B:], scale_table[:].indirect(offsets[:]))
-        late_scales = keep.tile([P, S], U8, name="late_scales", align_bytes=64)
-        for g in range(PASSES):
-            nc.vector.tensor_copy(picked_words[g][:, LEAD_W:].bitcast(U32), word_table[g][:].bitcast(U32).indirect(offsets[:]))
-            product(0, g, picked_words[g][:, LEAD_W:], picked_scales[:, LEAD_B:])
-            if g == 0:
-                nc.vector.tensor_copy(late_scales[:], picked_scales[:, LEAD_B - 1 : LEAD_B - 1 + S])
-            late = keep.tile([P, S], I32, name="late_words%d" % g, align_bytes=64)
-            nc.vector.tensor_copy(late[:], picked_words[g][:, LEAD_W - 1 : LEAD_W - 1 + S])
-            product(1, g, late[:], late_scales[:])
+        picked_scales = keep.tile([P, S], U8, name="picked_scales", align_bytes=64)
+        nc.vector.tensor_copy(picked_scales[:], scale_table[:].indirect(offsets[:]))
+
+        table1 = shared.tile([P, T], I32, name="table1", align_bytes=64, offset=4 * S)
+        nc.sync.dma_start(out=table1[:], in_=x_words[1].rearrange("p c r -> p (c r)").bitcast(I32))
+
+        picked0 = shared.tile([P, S], I32, name="picked0", align_bytes=64, offset=0)
+        nc.vector.tensor_copy(picked0[:].bitcast(U32), table0[:].bitcast(U32).indirect(offsets[:]))
+
+        w2_raw1 = keep.tile([P, PACK, N], F32, name="w2_raw1", tag="table0", align_bytes=64)
+        nc.sync.dma_start(out=w2_raw1[:], in_=w2[K_PASS:, :].rearrange("(p j) n -> p j n", j=PACK))
+
+        nc.vector.tensor_copy(late_scales[:, 1:], picked_scales[:, : S - 1])
+        product(quantize(w1_raw[:, 0], "10"), picked0, picked_scales, 0, True, False)
+        nc.vector.tensor_copy(late_words[0][:, 1:], picked0[:, : S - 1])
+        product(quantize(w2_raw0[:], "20"), late_words[0], late_scales, 0, False, False)
+
+        picked1 = keep.tile([P, S], I32, name="picked1", align_bytes=64)
+        nc.vector.tensor_copy(picked1[:].bitcast(U32), table1[:].bitcast(U32).indirect(offsets[:]))
+        product(quantize(w1_raw[:, 1], "11"), picked1, picked_scales, 1, False, False)
+        nc.vector.tensor_copy(late_words[1][:, 1:], picked1[:, : S - 1])
+        product(quantize(w2_raw1[:], "21"), late_words[1], late_scales, 1, False, True)
 
         result0 = keep.tile([N, HALF], F32, name="result0")
         nc.vector.tensor_scalar_max(result0[:], acc[0][:], 0.0)

@@ -32,40 +32,58 @@ def tile_picked_listconv_relu_p_kernel(tc, x_words, x_scales, w1, w2, offs, out)
         keep = ctx.enter_context(tc.tile_pool(name="keep", bufs=1))
         shared = ctx.enter_context(tc.tile_pool(name="shared", bufs=1))
         psum = ctx.enter_context(tc.psum_pool(name="psum", bufs=1))
+        raw_bytes = PACK * N * 4
+
+        def load_words(table, g):
+            nc.sync.dma_start(out=table[:], in_=x_words[g].rearrange("p c r -> p (c r)").bitcast(I32))
+
+        def load_weight(raw, w, g):
+            nc.sync.dma_start(out=raw[:], in_=w[g * K_PASS : (g + 1) * K_PASS, :].rearrange("(p j) n -> p j n", j=PACK))
 
         offsets = lists.tile([P, S // 16], U16, name="offsets")
+        table0 = keep.tile([P, T], I32, name="table0", align_bytes=64)
+        load_words(table0, 0)
         nc.sync.dma_start(offsets[:], offs)
+        raw10 = keep.tile([P, PACK, N], F32, name="raw10", align_bytes=64)
+        load_weight(raw10, w1, 0)
 
-        scale_table = shared.tile([P, T], U8, name="scale_table", align_bytes=64, offset=4 * S - T // 2)
+        scale_table = keep.tile([P, T], U8, name="scale_table", align_bytes=64)
         nc.vector.memset(scale_table[:].bitcast(I32), 0)
         for q in range(P // QUAD):
-            nc.scalar.dma_start(
+            nc.sync.dma_start(
                 out=scale_table[QUAD * q : QUAD * q + PASSES * SROWS, :].bitcast(I32),
                 in_=x_scales[:, SROWS * q : SROWS * (q + 1), :].bitcast(I32),
             )
 
-        table0 = keep.tile([P, T], I32, name="table0", tag="table0", align_bytes=64)
-        nc.sync.dma_start(out=table0[:], in_=x_words[0].rearrange("p c r -> p (c r)").bitcast(I32))
-        w1_raw = keep.tile([P, PASSES, PACK, N], F32, name="w1_raw")
-        nc.sync.dma_start(out=w1_raw[:], in_=w1.rearrange("(g p j) n -> p g j n", j=PACK, p=P))
-        w2_raw0 = keep.tile([P, PACK, N], F32, name="w2_raw0")
-        nc.sync.dma_start(out=w2_raw0[:], in_=w2[:K_PASS, :].rearrange("(p j) n -> p j n", j=PACK))
-
         late_scales = keep.tile([P, S], U8, name="late_scales", align_bytes=64)
-        nc.vector.memset(late_scales[:, :4].bitcast(I32), 0)
-        late_words = []
-        for g in range(PASSES):
-            late = keep.tile([P, S], I32, name="late_words%d" % g, align_bytes=64)
-            nc.vector.memset(late[:, :1], 0)
-            late_words.append(late)
+        late1 = keep.tile([P, S], I32, name="late1", align_bytes=64)
+        heads = [late_scales[:, :8].bitcast(I32), late1[:, :2]]
+        blanks = []
+        for i in range(2):
+            blank = shared.tile([P, 32], I32, name="blank%d" % i, align_bytes=64, offset=(2 * i + 1) * raw_bytes - 64)
+            nc.vector.memset(blank[:, 15:17], 0)
+            blanks.append(blank)
+        picked0 = keep.tile([P, LEAD_W + S], I32, name="picked0", align_bytes=64)
+        nc.vector.memset(picked0[:, :LEAD_W], 0)
+        for i in range(2):
+            nc.vector.tensor_copy(heads[i], blanks[i][:, 15:17])
+
+        raw20 = shared.tile([P, PACK, N], F32, name="raw20", align_bytes=64, offset=0)
+        load_weight(raw20, w2, 0)
+        raw11 = shared.tile([P, PACK, N], F32, name="raw11", align_bytes=64, offset=raw_bytes)
+        load_weight(raw11, w1, 1)
+        raw21 = shared.tile([P, PACK, N], F32, name="raw21", align_bytes=64, offset=2 * raw_bytes)
+        load_weight(raw21, w2, 1)
+        table1 = shared.tile([P, T], I32, name="table1", align_bytes=64, offset=3 * raw_bytes)
+        load_words(table1, 1)
 
         acc = [psum.tile([N, HALF], F32, name="acc%d" % h) for h in range(2)]
 
-        def quantize(raw, label):
-            grouped = keep.tile([P, N, PACK], BF16, name="grouped" + label, align_bytes=64)
+        def quantize(raw, label, tag):
+            grouped = keep.tile([P, N, PACK], BF16, name="grouped" + label, tag=tag, align_bytes=64)
             nc.scalar.activation(
                 grouped[:].rearrange("p (c i) t -> p c t i", i=4),
-                raw.rearrange("p t (c i) -> p c t i", i=4),
+                raw[:].rearrange("p t (c i) -> p c t i", i=4),
                 ACT.Copy,
             )
             codes = keep.tile([P, N], U32, name="codes" + label, align_bytes=64)
@@ -73,45 +91,49 @@ def tile_picked_listconv_relu_p_kernel(tc, x_words, x_scales, w1, w2, offs, out)
             nc.vector.quantize_mx(out=codes[:].bitcast(FP8X4), scales=scales[:], in_=grouped[:].rearrange("p n t -> p (n t)"))
             return codes, scales
 
-        def product(stationary, words, planes, g, start, stop):
+        def product(stationary, words, planes, g, h, start, stop):
             codes, scales = stationary
-            for h in range(2):
-                nc.tensor.matmul_mx(
-                    out=acc[h][:],
-                    lhsT=codes[:].bitcast(FP8X4),
-                    lhsT_scale=scales[:],
-                    rhs=words[:, h * HALF : (h + 1) * HALF].bitcast(FP8X4),
-                    rhs_scale=planes[SROWS * g :, h * HALF : (h + 1) * HALF],
-                    start=start,
-                    stop=stop,
-                )
+            nc.tensor.matmul_mx(
+                out=acc[h][:],
+                lhsT=codes[:].bitcast(FP8X4),
+                lhsT_scale=scales[:],
+                rhs=words[:, h * HALF : (h + 1) * HALF].bitcast(FP8X4),
+                rhs_scale=planes[SROWS * g :, h * HALF : (h + 1) * HALF],
+                start=start,
+                stop=stop,
+            )
 
+        nc.vector.tensor_copy(picked0[:, LEAD_W:].bitcast(U32), table0[:].bitcast(U32).indirect(offsets[:]))
+        w10 = quantize(raw10, "10", "g10")
         picked_scales = keep.tile([P, S], U8, name="picked_scales", align_bytes=64)
         nc.vector.tensor_copy(picked_scales[:], scale_table[:].indirect(offsets[:]))
+        for h in range(2):
+            product(w10, picked0[:, LEAD_W:], picked_scales, 0, h, True, False)
 
-        table1 = shared.tile([P, T], I32, name="table1", align_bytes=64, offset=4 * S)
-        nc.sync.dma_start(out=table1[:], in_=x_words[1].rearrange("p c r -> p (c r)").bitcast(I32))
-
-        picked0 = shared.tile([P, S], I32, name="picked0", align_bytes=64, offset=0)
-        nc.vector.tensor_copy(picked0[:].bitcast(U32), table0[:].bitcast(U32).indirect(offsets[:]))
-
-        w2_raw1 = keep.tile([P, PACK, N], F32, name="w2_raw1", tag="table0", align_bytes=64)
-        nc.sync.dma_start(out=w2_raw1[:], in_=w2[K_PASS:, :].rearrange("(p j) n -> p j n", j=PACK))
-
+        late0 = keep.tile([P, S], I32, name="late0", tag="g10", align_bytes=64)
+        nc.vector.tensor_copy(late0[:], picked0[:, LEAD_W - 1 : LEAD_W - 1 + S])
+        w20 = quantize(raw20, "20", "g20")
         nc.vector.tensor_copy(late_scales[:, 1:], picked_scales[:, : S - 1])
-        product(quantize(w1_raw[:, 0], "10"), picked0, picked_scales, 0, True, False)
-        nc.vector.tensor_copy(late_words[0][:, 1:], picked0[:, : S - 1])
-        product(quantize(w2_raw0[:], "20"), late_words[0], late_scales, 0, False, False)
+        for h in range(2):
+            product(w20, late0, late_scales, 0, h, False, False)
 
+        w11 = quantize(raw11, "11", "g11")
+        w21 = quantize(raw21, "21", "g21")
         picked1 = keep.tile([P, S], I32, name="picked1", align_bytes=64)
-        nc.vector.tensor_copy(picked1[:].bitcast(U32), table1[:].bitcast(U32).indirect(offsets[:]))
-        product(quantize(w1_raw[:, 1], "11"), picked1, picked_scales, 1, False, False)
-        nc.vector.tensor_copy(late_words[1][:, 1:], picked1[:, : S - 1])
-        product(quantize(w2_raw1[:], "21"), late_words[1], late_scales, 1, False, True)
+        for h in range(2):
+            nc.vector.tensor_copy(
+                picked1[:, h * HALF : (h + 1) * HALF].bitcast(U32),
+                table1[:].bitcast(U32).indirect(offsets[:, h * HALF // 16 : (h + 1) * HALF // 16]),
+            )
+            product(w11, picked1, picked_scales, 1, h, False, False)
+        nc.vector.tensor_copy(late1[:, 1:HALF], picked1[:, : HALF - 1])
+        product(w21, late1, late_scales, 1, 0, False, True)
+        nc.vector.tensor_copy(late1[:, HALF:], picked1[:, HALF - 1 : S - 1])
+        product(w21, late1, late_scales, 1, 1, False, True)
 
         result0 = keep.tile([N, HALF], F32, name="result0")
-        nc.vector.tensor_scalar_max(result0[:], acc[0][:], 0.0)
-        nc.sync.dma_start(out=out[:, :HALF], in_=result0[:])
+        nc.scalar.activation(result0[:], acc[0][:], ACT.Relu)
+        nc.scalar.dma_start(out=out[:, :HALF], in_=result0[:])
         result1 = keep.tile([N, HALF], F32, name="result1")
-        nc.scalar.activation(result1[:], acc[1][:], ACT.Relu)
-        nc.scalar.dma_start(out=out[:, HALF:], in_=result1[:])
+        nc.vector.tensor_scalar_max(result1[:], acc[1][:], 0.0)
+        nc.sync.dma_start(out=out[:, HALF:], in_=result1[:])

@@ -32,55 +32,50 @@ def tile_picked_listconv_relu_p_kernel(tc, x_words, x_scales, w1, w2, offs, out)
         keep = ctx.enter_context(tc.tile_pool(name="keep", bufs=1))
         shared = ctx.enter_context(tc.tile_pool(name="shared", bufs=1))
         psum = ctx.enter_context(tc.psum_pool(name="psum", bufs=1))
-        raw_bytes = PACK * N * 4
+        unit = PACK * N * 4
 
-        def load_words(table, g):
+        def load_words(g, place):
+            table = shared.tile([P, T], I32, name="table%d" % g, align_bytes=64, offset=place * unit)
             nc.sync.dma_start(out=table[:], in_=x_words[g].rearrange("p c r -> p (c r)").bitcast(I32))
+            return table
 
-        def load_weight(raw, w, g):
+        def load_weight(w, g, label, place):
+            raw = shared.tile([P, PACK, N], F32, name="raw" + label, align_bytes=64, offset=place * unit)
             nc.sync.dma_start(out=raw[:], in_=w[g * K_PASS : (g + 1) * K_PASS, :].rearrange("(p j) n -> p j n", j=PACK))
+            return raw
 
         offsets = lists.tile([P, S // 16], U16, name="offsets")
-        table0 = keep.tile([P, T], I32, name="table0", align_bytes=64)
-        load_words(table0, 0)
         nc.sync.dma_start(offsets[:], offs)
-        raw10 = keep.tile([P, PACK, N], F32, name="raw10", align_bytes=64)
-        load_weight(raw10, w1, 0)
 
         scale_table = keep.tile([P, T], U8, name="scale_table", align_bytes=64)
         nc.vector.memset(scale_table[:].bitcast(I32), 0)
         for q in range(P // QUAD):
-            nc.sync.dma_start(
+            queue = nc.sync if q % 2 == 0 else nc.scalar
+            queue.dma_start(
                 out=scale_table[QUAD * q : QUAD * q + PASSES * SROWS, :].bitcast(I32),
                 in_=x_scales[:, SROWS * q : SROWS * (q + 1), :].bitcast(I32),
             )
 
-        late_scales = keep.tile([P, S], U8, name="late_scales", align_bytes=64)
-        late1 = keep.tile([P, S], I32, name="late1", align_bytes=64)
-        heads = [late_scales[:, :8].bitcast(I32), late1[:, :2]]
-        blanks = []
-        for i in range(2):
-            blank = shared.tile([P, 32], I32, name="blank%d" % i, align_bytes=64, offset=(2 * i + 1) * raw_bytes - 64)
-            nc.vector.memset(blank[:, 15:17], 0)
-            blanks.append(blank)
+        blank = shared.tile([P, 8 * unit // 4], I32, name="blank", align_bytes=64, offset=0)
+        nc.vector.memset(blank[:, :1], 0)
+        picked_scales = keep.tile([P, LEAD_B + S], U8, name="picked_scales", align_bytes=64)
+        nc.vector.memset(picked_scales[:, :LEAD_B].bitcast(I32), 0)
+        late1a = keep.tile([P, HALF], I32, name="late1a", align_bytes=64)
+        nc.vector.tensor_copy(late1a[:, :1], blank[:, :1])
         picked0 = keep.tile([P, LEAD_W + S], I32, name="picked0", align_bytes=64)
         nc.vector.memset(picked0[:, :LEAD_W], 0)
-        for i in range(2):
-            nc.vector.tensor_copy(heads[i], blanks[i][:, 15:17])
 
-        raw20 = shared.tile([P, PACK, N], F32, name="raw20", align_bytes=64, offset=0)
-        load_weight(raw20, w2, 0)
-        raw11 = shared.tile([P, PACK, N], F32, name="raw11", align_bytes=64, offset=raw_bytes)
-        load_weight(raw11, w1, 1)
-        raw21 = shared.tile([P, PACK, N], F32, name="raw21", align_bytes=64, offset=2 * raw_bytes)
-        load_weight(raw21, w2, 1)
-        table1 = shared.tile([P, T], I32, name="table1", align_bytes=64, offset=3 * raw_bytes)
-        load_words(table1, 1)
+        table0 = load_words(0, 0)
+        raw10 = load_weight(w1, 0, "10", 2)
+        raw20 = load_weight(w2, 0, "20", 3)
+        raw11 = load_weight(w1, 1, "11", 4)
+        table1 = load_words(1, 5)
+        raw21 = load_weight(w2, 1, "21", 7)
 
         acc = [psum.tile([N, HALF], F32, name="acc%d" % h) for h in range(2)]
 
-        def quantize(raw, label, tag):
-            grouped = keep.tile([P, N, PACK], BF16, name="grouped" + label, tag=tag, align_bytes=64)
+        def quantize(raw, label):
+            grouped = keep.tile([P, N, PACK], BF16, name="grouped" + label, align_bytes=64)
             nc.scalar.activation(
                 grouped[:].rearrange("p (c i) t -> p c t i", i=4),
                 raw[:].rearrange("p t (c i) -> p c t i", i=4),
@@ -97,39 +92,40 @@ def tile_picked_listconv_relu_p_kernel(tc, x_words, x_scales, w1, w2, offs, out)
                 out=acc[h][:],
                 lhsT=codes[:].bitcast(FP8X4),
                 lhsT_scale=scales[:],
-                rhs=words[:, h * HALF : (h + 1) * HALF].bitcast(FP8X4),
+                rhs=words.bitcast(FP8X4),
                 rhs_scale=planes[SROWS * g :, h * HALF : (h + 1) * HALF],
                 start=start,
                 stop=stop,
             )
 
+        nc.vector.tensor_copy(picked_scales[:, LEAD_B:], scale_table[:].indirect(offsets[:]))
         nc.vector.tensor_copy(picked0[:, LEAD_W:].bitcast(U32), table0[:].bitcast(U32).indirect(offsets[:]))
-        w10 = quantize(raw10, "10", "g10")
-        picked_scales = keep.tile([P, S], U8, name="picked_scales", align_bytes=64)
-        nc.vector.tensor_copy(picked_scales[:], scale_table[:].indirect(offsets[:]))
+        w10 = quantize(raw10, "10")
         for h in range(2):
-            product(w10, picked0[:, LEAD_W:], picked_scales, 0, h, True, False)
+            product(w10, picked0[:, LEAD_W + h * HALF : LEAD_W + (h + 1) * HALF], picked_scales[:, LEAD_B:], 0, h, True, False)
 
-        late0 = keep.tile([P, S], I32, name="late0", tag="g10", align_bytes=64)
+        late_scales = shared.tile([P, S], U8, name="late_scales", align_bytes=64, offset=2 * unit + S)
+        nc.vector.tensor_copy(late_scales[:], picked_scales[:, LEAD_B - 1 : LEAD_B - 1 + S])
+        late0 = shared.tile([P, S], I32, name="late0", align_bytes=64, offset=unit + S)
         nc.vector.tensor_copy(late0[:], picked0[:, LEAD_W - 1 : LEAD_W - 1 + S])
-        w20 = quantize(raw20, "20", "g20")
-        nc.vector.tensor_copy(late_scales[:, 1:], picked_scales[:, : S - 1])
+        w20 = quantize(raw20, "20")
         for h in range(2):
-            product(w20, late0, late_scales, 0, h, False, False)
+            product(w20, late0[:, h * HALF : (h + 1) * HALF], late_scales, 0, h, False, False)
 
-        w11 = quantize(raw11, "11", "g11")
-        w21 = quantize(raw21, "21", "g21")
+        w11 = quantize(raw11, "11")
         picked1 = keep.tile([P, S], I32, name="picked1", align_bytes=64)
         for h in range(2):
             nc.vector.tensor_copy(
                 picked1[:, h * HALF : (h + 1) * HALF].bitcast(U32),
                 table1[:].bitcast(U32).indirect(offsets[:, h * HALF // 16 : (h + 1) * HALF // 16]),
             )
-            product(w11, picked1, picked_scales, 1, h, False, False)
-        nc.vector.tensor_copy(late1[:, 1:HALF], picked1[:, : HALF - 1])
-        product(w21, late1, late_scales, 1, 0, False, True)
-        nc.vector.tensor_copy(late1[:, HALF:], picked1[:, HALF - 1 : S - 1])
-        product(w21, late1, late_scales, 1, 1, False, True)
+            product(w11, picked1[:, h * HALF : (h + 1) * HALF], picked_scales[:, LEAD_B:], 1, h, False, False)
+        nc.vector.tensor_copy(late1a[:, 1:], picked1[:, : HALF - 1])
+        w21 = quantize(raw21, "21")
+        product(w21, late1a[:], late_scales, 1, 0, False, True)
+        late1b = shared.tile([P, HALF], I32, name="late1b", align_bytes=64, offset=7 * unit)
+        nc.vector.tensor_copy(late1b[:], picked1[:, HALF - 1 : S - 1])
+        product(w21, late1b[:], late_scales, 1, 1, False, True)
 
         result0 = keep.tile([N, HALF], F32, name="result0")
         nc.scalar.activation(result0[:], acc[0][:], ACT.Relu)

@@ -18,11 +18,14 @@ P = 128
 PACK = 4
 K_PASS = P * PACK
 PASSES = K // K_PASS
-QUAD = 32
-SROWS = 4
-LEAD_W = 16
-LEAD_B = 64
+QUADRANT = 32
+SCALE_ROWS = 4
+LIST_ROWS = 16
+LEAD_WORDS = 16
+LEAD_BYTES = 64
+LINE = 4
 HALF = S // 2
+RAW_BYTES = PACK * N * 4
 
 
 def tile_picked_listconv_relu_p_kernel(tc, x_words, x_scales, w1, w2, offs, out):
@@ -30,102 +33,103 @@ def tile_picked_listconv_relu_p_kernel(tc, x_words, x_scales, w1, w2, offs, out)
     with ExitStack() as ctx:
         lists = ctx.enter_context(tc.tile_pool(name="lists", bufs=1))
         keep = ctx.enter_context(tc.tile_pool(name="keep", bufs=1))
-        shared = ctx.enter_context(tc.tile_pool(name="shared", bufs=1))
+        placed = ctx.enter_context(tc.tile_pool(name="placed", bufs=1))
         psum = ctx.enter_context(tc.psum_pool(name="psum", bufs=1))
-        unit = PACK * N * 4
 
-        def load_words(g, place):
-            table = shared.tile([P, T], I32, name="table%d" % g, align_bytes=64, offset=place * unit)
+        def load_words(table, g):
             nc.sync.dma_start(out=table[:], in_=x_words[g].rearrange("p c r -> p (c r)").bitcast(I32))
-            return table
 
-        def load_weight(w, g, label, place):
-            raw = shared.tile([P, PACK, N], F32, name="raw" + label, align_bytes=64, offset=place * unit)
-            nc.sync.dma_start(out=raw[:], in_=w[g * K_PASS : (g + 1) * K_PASS, :].rearrange("(p j) n -> p j n", j=PACK))
-            return raw
+        def load_weights(raw, w, g):
+            nc.sync.dma_start(out=raw[:], in_=w[g * K_PASS : (g + 1) * K_PASS, :].rearrange("(p t) n -> p t n", t=PACK))
 
-        offsets = lists.tile([P, S // 16], U16, name="offsets")
+        offsets = lists.tile([P, S // LIST_ROWS], U16, name="offsets")
         nc.sync.dma_start(offsets[:], offs)
+        table0 = keep.tile([P, T], I32, name="table0", align_bytes=64)
+        load_words(table0, 0)
+        w1_raw0 = keep.tile([P, PACK, N], F32, name="w1_raw0", align_bytes=64)
+        load_weights(w1_raw0, w1, 0)
 
         scale_table = keep.tile([P, T], U8, name="scale_table", align_bytes=64)
         nc.vector.memset(scale_table[:].bitcast(I32), 0)
-        for q in range(P // QUAD):
-            queue = nc.sync if q % 2 == 0 else nc.scalar
-            queue.dma_start(
-                out=scale_table[QUAD * q : QUAD * q + PASSES * SROWS, :].bitcast(I32),
-                in_=x_scales[:, SROWS * q : SROWS * (q + 1), :].bitcast(I32),
+        for q in range(P // QUADRANT):
+            nc.sync.dma_start(
+                out=scale_table[QUADRANT * q : QUADRANT * q + PASSES * SCALE_ROWS, :].bitcast(I32),
+                in_=x_scales[:, SCALE_ROWS * q : SCALE_ROWS * (q + 1), :].bitcast(I32),
             )
 
-        blank = shared.tile([P, 8 * unit // 4], I32, name="blank", align_bytes=64, offset=0)
-        nc.vector.memset(blank[:, :1], 0)
-        picked_scales = keep.tile([P, LEAD_B + S], U8, name="picked_scales", align_bytes=64)
-        nc.vector.memset(picked_scales[:, :LEAD_B].bitcast(I32), 0)
-        late1a = keep.tile([P, HALF], I32, name="late1a", align_bytes=64)
-        nc.vector.tensor_copy(late1a[:, :1], blank[:, :1])
-        picked0 = keep.tile([P, LEAD_W + S], I32, name="picked0", align_bytes=64)
-        nc.vector.memset(picked0[:, :LEAD_W], 0)
+        zero = placed.tile([P, 5 * RAW_BYTES // 4], I32, name="zero", align_bytes=64, offset=0)
+        nc.vector.memset(zero[:, :1], 0)
+        picked_scales = keep.tile([P, LEAD_BYTES + S], U8, name="picked_scales", align_bytes=64)
+        nc.vector.memset(picked_scales[:, :LEAD_BYTES].bitcast(I32), 0)
+        shifted1_first = keep.tile([P, HALF], I32, name="shifted1_first", align_bytes=64)
+        nc.vector.tensor_copy(shifted1_first[:, :1], zero[:, :1])
+        picked0 = keep.tile([P, LEAD_WORDS + S], I32, name="picked0", align_bytes=64)
+        nc.vector.memset(picked0[:, :LEAD_WORDS], 0)
 
-        table0 = load_words(0, 0)
-        raw10 = load_weight(w1, 0, "10", 2)
-        raw20 = load_weight(w2, 0, "20", 3)
-        raw11 = load_weight(w1, 1, "11", 4)
-        table1 = load_words(1, 5)
-        raw21 = load_weight(w2, 1, "21", 7)
+        w2_raw0 = placed.tile([P, PACK, N], F32, name="w2_raw0", align_bytes=64, offset=0)
+        load_weights(w2_raw0, w2, 0)
+        w1_raw1 = placed.tile([P, PACK, N], F32, name="w1_raw1", align_bytes=64, offset=RAW_BYTES)
+        load_weights(w1_raw1, w1, 1)
+        table1 = placed.tile([P, T], I32, name="table1", align_bytes=64, offset=2 * RAW_BYTES)
+        load_words(table1, 1)
+        w2_raw1 = placed.tile([P, PACK, N], F32, name="w2_raw1", align_bytes=64, offset=4 * RAW_BYTES)
+        load_weights(w2_raw1, w2, 1)
 
         acc = [psum.tile([N, HALF], F32, name="acc%d" % h) for h in range(2)]
 
         def quantize(raw, label):
-            grouped = keep.tile([P, N, PACK], BF16, name="grouped" + label, align_bytes=64)
+            grouped = keep.tile([P, N, PACK], BF16, name="grouped_" + label, tag="grouped_" + label, align_bytes=64)
             nc.scalar.activation(
-                grouped[:].rearrange("p (c i) t -> p c t i", i=4),
-                raw[:].rearrange("p t (c i) -> p c t i", i=4),
+                grouped[:].rearrange("p (c i) t -> p c t i", i=LINE),
+                raw[:].rearrange("p t (c i) -> p c t i", i=LINE),
                 ACT.Copy,
             )
-            codes = keep.tile([P, N], U32, name="codes" + label, align_bytes=64)
-            scales = keep.tile([P, N], U8, name="scales" + label, align_bytes=64)
+            codes = keep.tile([P, N], U32, name="codes_" + label, align_bytes=64)
+            scales = keep.tile([P, N], U8, name="scales_" + label, align_bytes=64)
             nc.vector.quantize_mx(out=codes[:].bitcast(FP8X4), scales=scales[:], in_=grouped[:].rearrange("p n t -> p (n t)"))
             return codes, scales
 
-        def product(stationary, words, planes, g, h, start, stop):
-            codes, scales = stationary
+        def product(weights, words, token_scales, g, h, start, stop):
+            codes, scales = weights
             nc.tensor.matmul_mx(
                 out=acc[h][:],
                 lhsT=codes[:].bitcast(FP8X4),
                 lhsT_scale=scales[:],
                 rhs=words.bitcast(FP8X4),
-                rhs_scale=planes[SROWS * g :, h * HALF : (h + 1) * HALF],
+                rhs_scale=token_scales[SCALE_ROWS * g :, h * HALF : (h + 1) * HALF],
                 start=start,
                 stop=stop,
             )
 
-        nc.vector.tensor_copy(picked_scales[:, LEAD_B:], scale_table[:].indirect(offsets[:]))
-        nc.vector.tensor_copy(picked0[:, LEAD_W:].bitcast(U32), table0[:].bitcast(U32).indirect(offsets[:]))
-        w10 = quantize(raw10, "10")
+        nc.vector.tensor_copy(picked0[:, LEAD_WORDS:].bitcast(U32), table0[:].bitcast(U32).indirect(offsets[:]))
+        w1_mx0 = quantize(w1_raw0, "w1_0")
+        nc.vector.tensor_copy(picked_scales[:, LEAD_BYTES:], scale_table[:].indirect(offsets[:]))
         for h in range(2):
-            product(w10, picked0[:, LEAD_W + h * HALF : LEAD_W + (h + 1) * HALF], picked_scales[:, LEAD_B:], 0, h, True, False)
+            words = picked0[:, LEAD_WORDS + h * HALF : LEAD_WORDS + (h + 1) * HALF]
+            product(w1_mx0, words, picked_scales[:, LEAD_BYTES:], 0, h, True, False)
 
-        late_scales = shared.tile([P, S], U8, name="late_scales", align_bytes=64, offset=2 * unit + S)
-        nc.vector.tensor_copy(late_scales[:], picked_scales[:, LEAD_B - 1 : LEAD_B - 1 + S])
-        late0 = shared.tile([P, S], I32, name="late0", align_bytes=64, offset=unit + S)
-        nc.vector.tensor_copy(late0[:], picked0[:, LEAD_W - 1 : LEAD_W - 1 + S])
-        w20 = quantize(raw20, "20")
+        shifted0 = keep.tile([P, S], I32, name="shifted0", tag="grouped_w1_0", align_bytes=64)
+        nc.vector.tensor_copy(shifted0[:], picked0[:, LEAD_WORDS - 1 : LEAD_WORDS - 1 + S])
+        w2_mx0 = quantize(w2_raw0, "w2_0")
+        shifted_scales = keep.tile([P, S], U8, name="shifted_scales", align_bytes=64)
+        nc.vector.tensor_copy(shifted_scales[:], picked_scales[:, LEAD_BYTES - 1 : LEAD_BYTES - 1 + S])
         for h in range(2):
-            product(w20, late0[:, h * HALF : (h + 1) * HALF], late_scales, 0, h, False, False)
+            product(w2_mx0, shifted0[:, h * HALF : (h + 1) * HALF], shifted_scales, 0, h, False, False)
 
-        w11 = quantize(raw11, "11")
+        w1_mx1 = quantize(w1_raw1, "w1_1")
         picked1 = keep.tile([P, S], I32, name="picked1", align_bytes=64)
         for h in range(2):
             nc.vector.tensor_copy(
                 picked1[:, h * HALF : (h + 1) * HALF].bitcast(U32),
-                table1[:].bitcast(U32).indirect(offsets[:, h * HALF // 16 : (h + 1) * HALF // 16]),
+                table1[:].bitcast(U32).indirect(offsets[:, h * HALF // LIST_ROWS : (h + 1) * HALF // LIST_ROWS]),
             )
-            product(w11, picked1[:, h * HALF : (h + 1) * HALF], picked_scales[:, LEAD_B:], 1, h, False, False)
-        nc.vector.tensor_copy(late1a[:, 1:], picked1[:, : HALF - 1])
-        w21 = quantize(raw21, "21")
-        product(w21, late1a[:], late_scales, 1, 0, False, True)
-        late1b = shared.tile([P, HALF], I32, name="late1b", align_bytes=64, offset=7 * unit)
-        nc.vector.tensor_copy(late1b[:], picked1[:, HALF - 1 : S - 1])
-        product(w21, late1b[:], late_scales, 1, 1, False, True)
+            product(w1_mx1, picked1[:, h * HALF : (h + 1) * HALF], picked_scales[:, LEAD_BYTES:], 1, h, False, False)
+        nc.vector.tensor_copy(shifted1_first[:, 1:], picked1[:, : HALF - 1])
+        w2_mx1 = quantize(w2_raw1, "w2_1")
+        product(w2_mx1, shifted1_first[:], shifted_scales, 1, 0, False, True)
+        shifted1_second = placed.tile([P, HALF], I32, name="shifted1_second", align_bytes=64, offset=4 * RAW_BYTES)
+        nc.vector.tensor_copy(shifted1_second[:], picked1[:, HALF - 1 : S - 1])
+        product(w2_mx1, shifted1_second[:], shifted_scales, 1, 1, False, True)
 
         result0 = keep.tile([N, HALF], F32, name="result0")
         nc.scalar.activation(result0[:], acc[0][:], ACT.Relu)

@@ -43,11 +43,9 @@ def tile_picked_listconv_relu_p_kernel(tc, x_words, x_scales, w1, w2, offs, out)
             nc.sync.dma_start(out=raw[:], in_=w[g * K_PASS : (g + 1) * K_PASS, :].rearrange("(p t) n -> p t n", t=PACK))
 
         offsets = lists.tile([P, S // LIST_ROWS], U16, name="offsets")
-        nc.sync.dma_start(offsets[:], offs)
         table0 = keep.tile([P, T], I32, name="table0", align_bytes=64)
         load_words(table0, 0)
-        w1_raw0 = keep.tile([P, PACK, N], F32, name="w1_raw0", align_bytes=64)
-        load_weights(w1_raw0, w1, 0)
+        nc.sync.dma_start(offsets[:], offs)
 
         scale_table = keep.tile([P, T], U8, name="scale_table", align_bytes=64)
         nc.vector.memset(scale_table[:].bitcast(I32), 0)
@@ -57,7 +55,7 @@ def tile_picked_listconv_relu_p_kernel(tc, x_words, x_scales, w1, w2, offs, out)
                 in_=x_scales[:, SCALE_ROWS * q : SCALE_ROWS * (q + 1), :].bitcast(I32),
             )
 
-        zero = placed.tile([P, 5 * RAW_BYTES // 4], I32, name="zero", align_bytes=64, offset=0)
+        zero = placed.tile([P, 6 * RAW_BYTES // 4], I32, name="zero", align_bytes=64, offset=0)
         nc.vector.memset(zero[:, :1], 0)
         picked_scales = keep.tile([P, LEAD_BYTES + S], U8, name="picked_scales", align_bytes=64)
         nc.vector.memset(picked_scales[:, :LEAD_BYTES].bitcast(I32), 0)
@@ -66,6 +64,8 @@ def tile_picked_listconv_relu_p_kernel(tc, x_words, x_scales, w1, w2, offs, out)
         picked0 = keep.tile([P, LEAD_WORDS + S], I32, name="picked0", align_bytes=64)
         nc.vector.memset(picked0[:, :LEAD_WORDS], 0)
 
+        w1_raw0 = placed.tile([P, PACK, N], F32, name="w1_raw0", align_bytes=64, offset=5 * RAW_BYTES)
+        load_weights(w1_raw0, w1, 0)
         w2_raw0 = placed.tile([P, PACK, N], F32, name="w2_raw0", align_bytes=64, offset=0)
         load_weights(w2_raw0, w2, 0)
         w1_raw1 = placed.tile([P, PACK, N], F32, name="w1_raw1", align_bytes=64, offset=RAW_BYTES)
@@ -102,17 +102,16 @@ def tile_picked_listconv_relu_p_kernel(tc, x_words, x_scales, w1, w2, offs, out)
             )
 
         nc.vector.tensor_copy(picked0[:, LEAD_WORDS:].bitcast(U32), table0[:].bitcast(U32).indirect(offsets[:]))
-        w1_mx0 = quantize(w1_raw0, "w1_0")
         nc.vector.tensor_copy(picked_scales[:, LEAD_BYTES:], scale_table[:].indirect(offsets[:]))
+        w1_mx0 = quantize(w1_raw0, "w1_0")
         for h in range(2):
             words = picked0[:, LEAD_WORDS + h * HALF : LEAD_WORDS + (h + 1) * HALF]
             product(w1_mx0, words, picked_scales[:, LEAD_BYTES:], 0, h, True, False)
-
-        shifted0 = keep.tile([P, S], I32, name="shifted0", tag="grouped_w1_0", align_bytes=64)
+        shifted0 = placed.tile([P, S], I32, name="shifted0", align_bytes=64, offset=5 * RAW_BYTES)
         nc.vector.tensor_copy(shifted0[:], picked0[:, LEAD_WORDS - 1 : LEAD_WORDS - 1 + S])
-        w2_mx0 = quantize(w2_raw0, "w2_0")
-        shifted_scales = keep.tile([P, S], U8, name="shifted_scales", align_bytes=64)
+        shifted_scales = keep.tile([P, S], U8, name="shifted_scales", tag="grouped_w1_0", align_bytes=64)
         nc.vector.tensor_copy(shifted_scales[:], picked_scales[:, LEAD_BYTES - 1 : LEAD_BYTES - 1 + S])
+        w2_mx0 = quantize(w2_raw0, "w2_0")
         for h in range(2):
             product(w2_mx0, shifted0[:, h * HALF : (h + 1) * HALF], shifted_scales, 0, h, False, False)
 

@@ -25,6 +25,8 @@ LEAD_WORDS = 16
 LEAD_BYTES = 64
 LINE = 4
 HALF = S // 2
+FIRST_TOKENS = 256
+QUARTER = S // 4
 RAW_BYTES = PACK * N * 4
 
 
@@ -44,8 +46,10 @@ def tile_picked_listconv_relu_p_kernel(tc, x_words, x_scales, w1, w2, offs, out)
 
         offsets = lists.tile([P, S // LIST_ROWS], U16, name="offsets")
         table0 = keep.tile([P, T], I32, name="table0", align_bytes=64)
-        load_words(table0, 0)
+        words0 = x_words[0].rearrange("p c r -> p (c r)").bitcast(I32)
+        nc.sync.dma_start(out=table0[:, : FIRST_TOKENS], in_=words0[:, : FIRST_TOKENS])
         nc.sync.dma_start(offsets[:], offs)
+        nc.sync.dma_start(out=table0[:, FIRST_TOKENS :], in_=words0[:, FIRST_TOKENS :])
 
         scale_table = keep.tile([P, T], U8, name="scale_table", align_bytes=64)
         nc.vector.memset(scale_table[:].bitcast(I32), 0)
@@ -75,7 +79,8 @@ def tile_picked_listconv_relu_p_kernel(tc, x_words, x_scales, w1, w2, offs, out)
         w2_raw1 = placed.tile([P, PACK, N], F32, name="w2_raw1", align_bytes=64, offset=4 * RAW_BYTES)
         load_weights(w2_raw1, w2, 1)
 
-        acc = [psum.tile([N, HALF], F32, name="acc%d" % h) for h in range(2)]
+        pieces = [(first, QUARTER) for first in range(0, S, QUARTER)]
+        acc = [psum.tile([N, width], F32, name="acc%d" % h) for h, (first, width) in enumerate(pieces)]
 
         def quantize(raw, label):
             grouped = keep.tile([P, N, PACK], BF16, name="grouped_" + label, tag="grouped_" + label, align_bytes=64)
@@ -91,12 +96,13 @@ def tile_picked_listconv_relu_p_kernel(tc, x_words, x_scales, w1, w2, offs, out)
 
         def product(weights, words, token_scales, g, h, start, stop):
             codes, scales = weights
+            first, width = pieces[h]
             nc.tensor.matmul_mx(
                 out=acc[h][:],
                 lhsT=codes[:].bitcast(FP8X4),
                 lhsT_scale=scales[:],
                 rhs=words.bitcast(FP8X4),
-                rhs_scale=token_scales[SCALE_ROWS * g :, h * HALF : (h + 1) * HALF],
+                rhs_scale=token_scales[SCALE_ROWS * g :, first : first + width],
                 start=start,
                 stop=stop,
             )
@@ -104,35 +110,41 @@ def tile_picked_listconv_relu_p_kernel(tc, x_words, x_scales, w1, w2, offs, out)
         nc.vector.tensor_copy(picked0[:, LEAD_WORDS:].bitcast(U32), table0[:].bitcast(U32).indirect(offsets[:]))
         nc.vector.tensor_copy(picked_scales[:, LEAD_BYTES:], scale_table[:].indirect(offsets[:]))
         w1_mx0 = quantize(w1_raw0, "w1_0")
-        for h in range(2):
-            words = picked0[:, LEAD_WORDS + h * HALF : LEAD_WORDS + (h + 1) * HALF]
+        for h, (first, width) in enumerate(pieces):
+            words = picked0[:, LEAD_WORDS + first : LEAD_WORDS + first + width]
             product(w1_mx0, words, picked_scales[:, LEAD_BYTES:], 0, h, True, False)
         shifted0 = placed.tile([P, S], I32, name="shifted0", align_bytes=64, offset=5 * RAW_BYTES)
         nc.vector.tensor_copy(shifted0[:], picked0[:, LEAD_WORDS - 1 : LEAD_WORDS - 1 + S])
         shifted_scales = keep.tile([P, S], U8, name="shifted_scales", tag="grouped_w1_0", align_bytes=64)
         nc.vector.tensor_copy(shifted_scales[:], picked_scales[:, LEAD_BYTES - 1 : LEAD_BYTES - 1 + S])
         w2_mx0 = quantize(w2_raw0, "w2_0")
-        for h in range(2):
-            product(w2_mx0, shifted0[:, h * HALF : (h + 1) * HALF], shifted_scales, 0, h, False, False)
+        for h, (first, width) in enumerate(pieces):
+            product(w2_mx0, shifted0[:, first : first + width], shifted_scales, 0, h, False, False)
+
+        def gather1(picked, first, width):
+            nc.vector.tensor_copy(
+                picked.bitcast(U32), table1[:].bitcast(U32).indirect(offsets[:, first // LIST_ROWS : (first + width) // LIST_ROWS])
+            )
 
         w1_mx1 = quantize(w1_raw1, "w1_1")
         picked1 = keep.tile([P, S], I32, name="picked1", align_bytes=64)
-        for h in range(2):
-            nc.vector.tensor_copy(
-                picked1[:, h * HALF : (h + 1) * HALF].bitcast(U32),
-                table1[:].bitcast(U32).indirect(offsets[:, h * HALF // LIST_ROWS : (h + 1) * HALF // LIST_ROWS]),
-            )
-            product(w1_mx1, picked1[:, h * HALF : (h + 1) * HALF], picked_scales[:, LEAD_BYTES:], 1, h, False, False)
+        for first in (0, HALF):
+            gather1(picked1[:, first : first + HALF], first, HALF)
+        for h, (first, width) in enumerate(pieces):
+            product(w1_mx1, picked1[:, first : first + width], picked_scales[:, LEAD_BYTES:], 1, h, False, False)
         nc.vector.tensor_copy(shifted1_first[:, 1:], picked1[:, : HALF - 1])
         w2_mx1 = quantize(w2_raw1, "w2_1")
-        product(w2_mx1, shifted1_first[:], shifted_scales, 1, 0, False, True)
+        for h in (0, 1):
+            product(w2_mx1, shifted1_first[:, h * QUARTER : (h + 1) * QUARTER], shifted_scales, 1, h, False, True)
         shifted1_second = placed.tile([P, HALF], I32, name="shifted1_second", align_bytes=64, offset=4 * RAW_BYTES)
         nc.vector.tensor_copy(shifted1_second[:], picked1[:, HALF - 1 : S - 1])
-        product(w2_mx1, shifted1_second[:], shifted_scales, 1, 1, False, True)
+        for h in (0, 1):
+            product(w2_mx1, shifted1_second[:, h * QUARTER : (h + 1) * QUARTER], shifted_scales, 1, 2 + h, False, True)
 
-        result0 = keep.tile([N, HALF], F32, name="result0")
-        nc.scalar.activation(result0[:], acc[0][:], ACT.Relu)
-        nc.scalar.dma_start(out=out[:, :HALF], in_=result0[:])
-        result1 = keep.tile([N, HALF], F32, name="result1")
-        nc.vector.tensor_scalar_max(result1[:], acc[1][:], 0.0)
-        nc.sync.dma_start(out=out[:, HALF:], in_=result1[:])
+        result = [keep.tile([N, HALF], F32, name="result%d" % half) for half in range(2)]
+        nc.vector.tensor_scalar_max(result[0][:, :QUARTER], acc[0][:], 0.0)
+        nc.scalar.activation(result[0][:, QUARTER:], acc[1][:], ACT.Relu)
+        nc.sync.dma_start(out=out[:, :HALF], in_=result[0][:])
+        nc.scalar.activation(result[1][:, :QUARTER], acc[2][:], ACT.Relu)
+        nc.vector.tensor_scalar_max(result[1][:, QUARTER:], acc[3][:], 0.0)
+        nc.scalar.dma_start(out=out[:, HALF:], in_=result[1][:])

@@ -65,8 +65,8 @@ def tile_picked_listconv_relu_p_kernel(tc, x_words, x_scales, w1, w2, offs, out)
         nc.vector.memset(picked_scales[:, :LEAD_BYTES].bitcast(I32), 0)
         shifted1_first = keep.tile([P, HALF], I32, name="shifted1_first", align_bytes=64)
         nc.vector.tensor_copy(shifted1_first[:, :1], zero[:, :1])
-        picked0 = keep.tile([P, LEAD_WORDS + S], I32, name="picked0", align_bytes=64)
-        nc.vector.memset(picked0[:, :LEAD_WORDS], 0)
+        picked0_first = keep.tile([P, S], I32, name="picked0_first", align_bytes=64)
+        nc.vector.memset(picked0_first[:, :HALF], 0)
 
         w1_raw0 = placed.tile([P, PACK, N], F32, name="w1_raw0", align_bytes=64, offset=5 * RAW_BYTES)
         load_weights(w1_raw0, w1, 0)
@@ -107,17 +107,33 @@ def tile_picked_listconv_relu_p_kernel(tc, x_words, x_scales, w1, w2, offs, out)
                 stop=stop,
             )
 
-        nc.vector.tensor_copy(picked0[:, LEAD_WORDS:].bitcast(U32), table0[:].bitcast(U32).indirect(offsets[:]))
+        nc.vector.tensor_copy(picked0_first[:, HALF:].bitcast(U32), table0[:].bitcast(U32).indirect(offsets[:, : HALF // LIST_ROWS]))
         nc.vector.tensor_copy(picked_scales[:, LEAD_BYTES:], scale_table[:].indirect(offsets[:]))
         w1_mx0 = quantize(w1_raw0, "w1_0")
-        for h, (first, width) in enumerate(pieces):
-            words = picked0[:, LEAD_WORDS + first : LEAD_WORDS + first + width]
+        for h in (0, 1):
+            words = picked0_first[:, HALF + h * QUARTER : HALF + (h + 1) * QUARTER]
             product(w1_mx0, words, picked_scales[:, LEAD_BYTES:], 0, h, True, False)
-        shifted0 = placed.tile([P, S], I32, name="shifted0", align_bytes=64, offset=5 * RAW_BYTES)
-        nc.vector.tensor_copy(shifted0[:], picked0[:, LEAD_WORDS - 1 : LEAD_WORDS - 1 + S])
+        unread = psum.tile([N, S], F32, name="unread")
+        nc.tensor.matmul_mx(
+            out=unread[:],
+            lhsT=w1_mx0[0][:].bitcast(FP8X4),
+            lhsT_scale=w1_mx0[1][:],
+            rhs=picked0_first[:].bitcast(FP8X4),
+            rhs_scale=picked_scales[:, LEAD_BYTES:],
+            start=True,
+            stop=True,
+        )
+        picked0_second = placed.tile([P, HALF], I32, name="picked0_second", align_bytes=64, offset=5 * RAW_BYTES)
+        nc.vector.tensor_copy(picked0_second[:].bitcast(U32), table0[:].bitcast(U32).indirect(offsets[:, HALF // LIST_ROWS :]))
+        for h in (0, 1):
+            words = picked0_second[:, h * QUARTER : (h + 1) * QUARTER]
+            product(w1_mx0, words, picked_scales[:, LEAD_BYTES:], 0, 2 + h, True, False)
         shifted_scales = keep.tile([P, S], U8, name="shifted_scales", tag="grouped_w1_0", align_bytes=64)
         nc.vector.tensor_copy(shifted_scales[:], picked_scales[:, LEAD_BYTES - 1 : LEAD_BYTES - 1 + S])
+        shifted0 = placed.tile([P, S], I32, name="shifted0", align_bytes=64, offset=5 * RAW_BYTES + 4 * HALF)
+        nc.vector.tensor_copy(shifted0[:, : HALF + 1], picked0_first[:, HALF - 1 :])
         w2_mx0 = quantize(w2_raw0, "w2_0")
+        nc.vector.tensor_copy(shifted0[:, HALF + 1 :], picked0_second[:, : HALF - 1])
         for h, (first, width) in enumerate(pieces):
             product(w2_mx0, shifted0[:, first : first + width], shifted_scales, 0, h, False, False)
 

@@ -65,8 +65,8 @@ def tile_picked_listconv_relu_p_kernel(tc, x_words, x_scales, w1, w2, offs, out)
         nc.vector.memset(picked_scales[:, :LEAD_BYTES].bitcast(I32), 0)
         shifted1_first = keep.tile([P, HALF], I32, name="shifted1_first", align_bytes=64)
         nc.vector.tensor_copy(shifted1_first[:, :1], zero[:, :1])
-        picked0_first = keep.tile([P, S], I32, name="picked0_first", align_bytes=64)
-        nc.vector.memset(picked0_first[:, :HALF], 0)
+        picked0_first = keep.tile([P, LEAD_WORDS + HALF], I32, name="picked0_first", align_bytes=64)
+        nc.vector.memset(picked0_first[:, :LEAD_WORDS], 0)
 
         w1_raw0 = placed.tile([P, PACK, N], F32, name="w1_raw0", align_bytes=64, offset=5 * RAW_BYTES)
         load_weights(w1_raw0, w1, 0)
@@ -107,22 +107,12 @@ def tile_picked_listconv_relu_p_kernel(tc, x_words, x_scales, w1, w2, offs, out)
                 stop=stop,
             )
 
-        nc.vector.tensor_copy(picked0_first[:, HALF:].bitcast(U32), table0[:].bitcast(U32).indirect(offsets[:, : HALF // LIST_ROWS]))
+        nc.vector.tensor_copy(picked0_first[:, LEAD_WORDS:].bitcast(U32), table0[:].bitcast(U32).indirect(offsets[:, : HALF // LIST_ROWS]))
         nc.vector.tensor_copy(picked_scales[:, LEAD_BYTES:], scale_table[:].indirect(offsets[:]))
         w1_mx0 = quantize(w1_raw0, "w1_0")
         for h in (0, 1):
-            words = picked0_first[:, HALF + h * QUARTER : HALF + (h + 1) * QUARTER]
+            words = picked0_first[:, LEAD_WORDS + h * QUARTER : LEAD_WORDS + (h + 1) * QUARTER]
             product(w1_mx0, words, picked_scales[:, LEAD_BYTES:], 0, h, True, False)
-        unread = psum.tile([N, S], F32, name="unread")
-        nc.tensor.matmul_mx(
-            out=unread[:],
-            lhsT=w1_mx0[0][:].bitcast(FP8X4),
-            lhsT_scale=w1_mx0[1][:],
-            rhs=picked0_first[:].bitcast(FP8X4),
-            rhs_scale=picked_scales[:, LEAD_BYTES:],
-            start=True,
-            stop=True,
-        )
         picked0_second = placed.tile([P, HALF], I32, name="picked0_second", align_bytes=64, offset=5 * RAW_BYTES)
         nc.vector.tensor_copy(picked0_second[:].bitcast(U32), table0[:].bitcast(U32).indirect(offsets[:, HALF // LIST_ROWS :]))
         for h in (0, 1):
@@ -131,7 +121,7 @@ def tile_picked_listconv_relu_p_kernel(tc, x_words, x_scales, w1, w2, offs, out)
         shifted_scales = keep.tile([P, S], U8, name="shifted_scales", tag="grouped_w1_0", align_bytes=64)
         nc.vector.tensor_copy(shifted_scales[:], picked_scales[:, LEAD_BYTES - 1 : LEAD_BYTES - 1 + S])
         shifted0 = placed.tile([P, S], I32, name="shifted0", align_bytes=64, offset=5 * RAW_BYTES + 4 * HALF)
-        nc.vector.tensor_copy(shifted0[:, : HALF + 1], picked0_first[:, HALF - 1 :])
+        nc.vector.tensor_copy(shifted0[:, : HALF + 1], picked0_first[:, LEAD_WORDS - 1 :])
         w2_mx0 = quantize(w2_raw0, "w2_0")
         nc.vector.tensor_copy(shifted0[:, HALF + 1 :], picked0_second[:, : HALF - 1])
         for h, (first, width) in enumerate(pieces):

@@ -61,12 +61,12 @@ def tile_picked_listconv_relu_p_kernel(tc, x_words, x_scales, w1, w2, offs, out)
 
         zero = placed.tile([P, 6 * RAW_BYTES // 4], I32, name="zero", align_bytes=64, offset=0)
         nc.vector.memset(zero[:, :1], 0)
-        picked_scales = keep.tile([P, LEAD_BYTES + S], U8, name="picked_scales", align_bytes=64)
-        nc.vector.memset(picked_scales[:, :LEAD_BYTES].bitcast(I32), 0)
+        scales_first = keep.tile([P, LEAD_BYTES + HALF], U8, name="scales_first", align_bytes=64)
+        nc.vector.memset(scales_first[:, :LEAD_BYTES].bitcast(I32), 0)
         shifted1_first = keep.tile([P, HALF], I32, name="shifted1_first", align_bytes=64)
         nc.vector.tensor_copy(shifted1_first[:, :1], zero[:, :1])
-        picked0_first = keep.tile([P, LEAD_WORDS + HALF], I32, name="picked0_first", align_bytes=64)
-        nc.vector.memset(picked0_first[:, :LEAD_WORDS], 0)
+        picked0 = keep.tile([P, LEAD_WORDS + S], I32, name="picked0", align_bytes=64)
+        nc.vector.memset(picked0[:, :LEAD_WORDS], 0)
 
         w1_raw0 = placed.tile([P, PACK, N], F32, name="w1_raw0", align_bytes=64, offset=5 * RAW_BYTES)
         load_weights(w1_raw0, w1, 0)
@@ -96,34 +96,33 @@ def tile_picked_listconv_relu_p_kernel(tc, x_words, x_scales, w1, w2, offs, out)
 
         def product(weights, words, token_scales, g, h, start, stop):
             codes, scales = weights
-            first, width = pieces[h]
             nc.tensor.matmul_mx(
                 out=acc[h][:],
                 lhsT=codes[:].bitcast(FP8X4),
                 lhsT_scale=scales[:],
                 rhs=words.bitcast(FP8X4),
-                rhs_scale=token_scales[SCALE_ROWS * g :, first : first + width],
+                rhs_scale=token_scales[h // 2][SCALE_ROWS * g :, h % 2 * QUARTER : (h % 2 + 1) * QUARTER],
                 start=start,
                 stop=stop,
             )
 
-        nc.vector.tensor_copy(picked0_first[:, LEAD_WORDS:].bitcast(U32), table0[:].bitcast(U32).indirect(offsets[:, : HALF // LIST_ROWS]))
-        nc.vector.tensor_copy(picked_scales[:, LEAD_BYTES:], scale_table[:].indirect(offsets[:]))
+        nc.vector.tensor_copy(picked0[:, LEAD_WORDS:].bitcast(U32), table0[:].bitcast(U32).indirect(offsets[:]))
+        nc.vector.tensor_copy(scales_first[:, LEAD_BYTES:], scale_table[:].indirect(offsets[:, : HALF // LIST_ROWS]))
         w1_mx0 = quantize(w1_raw0, "w1_0")
+        scales_second = placed.tile([P, HALF], U8, name="scales_second", align_bytes=64, offset=5 * RAW_BYTES)
+        picked_scales = [scales_first[:, LEAD_BYTES:], scales_second[:]]
         for h in (0, 1):
-            words = picked0_first[:, LEAD_WORDS + h * QUARTER : LEAD_WORDS + (h + 1) * QUARTER]
-            product(w1_mx0, words, picked_scales[:, LEAD_BYTES:], 0, h, True, False)
-        picked0_second = placed.tile([P, HALF], I32, name="picked0_second", align_bytes=64, offset=5 * RAW_BYTES)
-        nc.vector.tensor_copy(picked0_second[:].bitcast(U32), table0[:].bitcast(U32).indirect(offsets[:, HALF // LIST_ROWS :]))
-        for h in (0, 1):
-            words = picked0_second[:, h * QUARTER : (h + 1) * QUARTER]
-            product(w1_mx0, words, picked_scales[:, LEAD_BYTES:], 0, 2 + h, True, False)
-        shifted_scales = keep.tile([P, S], U8, name="shifted_scales", tag="grouped_w1_0", align_bytes=64)
-        nc.vector.tensor_copy(shifted_scales[:], picked_scales[:, LEAD_BYTES - 1 : LEAD_BYTES - 1 + S])
+            product(w1_mx0, picked0[:, LEAD_WORDS + h * QUARTER : LEAD_WORDS + (h + 1) * QUARTER], picked_scales, 0, h, True, False)
+        nc.vector.tensor_copy(scales_second[:], scale_table[:].indirect(offsets[:, HALF // LIST_ROWS :]))
+        for h in (2, 3):
+            product(w1_mx0, picked0[:, LEAD_WORDS + h * QUARTER : LEAD_WORDS + (h + 1) * QUARTER], picked_scales, 0, h, True, False)
+        shifted_all = placed.tile([P, S], U8, name="shifted_all", align_bytes=64, offset=5 * RAW_BYTES + HALF)
+        shifted_scales = [shifted_all[:, :HALF], shifted_all[:, HALF:]]
         shifted0 = placed.tile([P, S], I32, name="shifted0", align_bytes=64, offset=5 * RAW_BYTES + 4 * HALF)
-        nc.vector.tensor_copy(shifted0[:, : HALF + 1], picked0_first[:, LEAD_WORDS - 1 :])
+        nc.vector.tensor_copy(shifted0[:], picked0[:, LEAD_WORDS - 1 : LEAD_WORDS - 1 + S])
+        nc.vector.tensor_copy(shifted_all[:, : HALF + 1], scales_first[:, LEAD_BYTES - 1 :])
+        nc.vector.tensor_copy(shifted_all[:, HALF + 1 :], scales_second[:, : HALF - 1])
         w2_mx0 = quantize(w2_raw0, "w2_0")
-        nc.vector.tensor_copy(shifted0[:, HALF + 1 :], picked0_second[:, : HALF - 1])
         for h, (first, width) in enumerate(pieces):
             product(w2_mx0, shifted0[:, first : first + width], shifted_scales, 0, h, False, False)
 
@@ -137,7 +136,7 @@ def tile_picked_listconv_relu_p_kernel(tc, x_words, x_scales, w1, w2, offs, out)
         for first in (0, HALF):
             gather1(picked1[:, first : first + HALF], first, HALF)
         for h, (first, width) in enumerate(pieces):
-            product(w1_mx1, picked1[:, first : first + width], picked_scales[:, LEAD_BYTES:], 1, h, False, False)
+            product(w1_mx1, picked1[:, first : first + width], picked_scales, 1, h, False, False)
         nc.vector.tensor_copy(shifted1_first[:, 1:], picked1[:, : HALF - 1])
         w2_mx1 = quantize(w2_raw1, "w2_1")
         for h in (0, 1):

@@ -61,34 +61,43 @@ def tile_picked_listconv_relu_p_kernel(tc, x_words, x_scales, w1, w2, offs, out)
 
         zero = placed.tile([P, 6 * RAW_BYTES // 4], I32, name="zero", align_bytes=64, offset=0)
         nc.vector.memset(zero[:, :1], 0)
-        scales_first = keep.tile([P, LEAD_BYTES + HALF], U8, name="scales_first", align_bytes=64)
-        nc.vector.memset(scales_first[:, :LEAD_BYTES].bitcast(I32), 0)
+        scales_all = keep.tile([P, LEAD_BYTES + S], U8, name="scales_all", align_bytes=64)
+        nc.vector.memset(scales_all[:, :LEAD_BYTES].bitcast(I32), 0)
         shifted1_first = keep.tile([P, HALF], I32, name="shifted1_first", align_bytes=64)
         nc.vector.tensor_copy(shifted1_first[:, :1], zero[:, :1])
         picked0 = keep.tile([P, LEAD_WORDS + S], I32, name="picked0", align_bytes=64)
         nc.vector.memset(picked0[:, :LEAD_WORDS], 0)
 
-        w1_raw0 = placed.tile([P, PACK, N], F32, name="w1_raw0", align_bytes=64, offset=5 * RAW_BYTES)
+        w1_raw0 = placed.tile([P, PACK, N], F32, name="w1_raw0", align_bytes=64, offset=0)
         load_weights(w1_raw0, w1, 0)
-        w2_raw0 = placed.tile([P, PACK, N], F32, name="w2_raw0", align_bytes=64, offset=0)
+        w2_raw0 = placed.tile([P, PACK, N], F32, name="w2_raw0", align_bytes=64, offset=5 * RAW_BYTES)
         load_weights(w2_raw0, w2, 0)
         w1_raw1 = placed.tile([P, PACK, N], F32, name="w1_raw1", align_bytes=64, offset=RAW_BYTES)
         load_weights(w1_raw1, w1, 1)
         table1 = placed.tile([P, T], I32, name="table1", align_bytes=64, offset=2 * RAW_BYTES)
         load_words(table1, 1)
-        w2_raw1 = placed.tile([P, PACK, N], F32, name="w2_raw1", align_bytes=64, offset=4 * RAW_BYTES)
-        load_weights(w2_raw1, w2, 1)
+        w2_rows1 = w2[K_PASS:, :].rearrange("(p t) n -> p t n", t=PACK)
+        w2_raw1 = []
+        for u in range(2):
+            part = placed.tile([P, 2, N], F32, name="w2_raw1_%d" % u, align_bytes=64, offset=4 * RAW_BYTES + u * RAW_BYTES // 2)
+            nc.sync.dma_start(out=part[:], in_=w2_rows1[:, 2 * u : 2 * u + 2, :])
+            w2_raw1.append(part)
 
         pieces = [(first, QUARTER) for first in range(0, S, QUARTER)]
         acc = [psum.tile([N, width], F32, name="acc%d" % h) for h, (first, width) in enumerate(pieces)]
 
-        def quantize(raw, label):
+        def interleave(parts, label):
             grouped = keep.tile([P, N, PACK], BF16, name="grouped_" + label, tag="grouped_" + label, align_bytes=64)
-            nc.scalar.activation(
-                grouped[:].rearrange("p (c i) t -> p c t i", i=LINE),
-                raw[:].rearrange("p t (c i) -> p c t i", i=LINE),
-                ACT.Copy,
-            )
+            rows = PACK // len(parts)
+            for u, raw in enumerate(parts):
+                nc.scalar.activation(
+                    grouped[:, :, rows * u : rows * (u + 1)].rearrange("p (c i) t -> p c t i", i=LINE),
+                    raw[:].rearrange("p t (c i) -> p c t i", i=LINE),
+                    ACT.Copy,
+                )
+            return grouped
+
+        def quantize(grouped, label):
             codes = keep.tile([P, N], U32, name="codes_" + label, align_bytes=64)
             scales = keep.tile([P, N], U8, name="scales_" + label, align_bytes=64)
             nc.vector.quantize_mx(out=codes[:].bitcast(FP8X4), scales=scales[:], in_=grouped[:].rearrange("p n t -> p (n t)"))
@@ -107,22 +116,30 @@ def tile_picked_listconv_relu_p_kernel(tc, x_words, x_scales, w1, w2, offs, out)
             )
 
         nc.vector.tensor_copy(picked0[:, LEAD_WORDS:].bitcast(U32), table0[:].bitcast(U32).indirect(offsets[:]))
-        nc.vector.tensor_copy(scales_first[:, LEAD_BYTES:], scale_table[:].indirect(offsets[:, : HALF // LIST_ROWS]))
-        w1_mx0 = quantize(w1_raw0, "w1_0")
-        scales_second = placed.tile([P, HALF], U8, name="scales_second", align_bytes=64, offset=5 * RAW_BYTES)
-        picked_scales = [scales_first[:, LEAD_BYTES:], scales_second[:]]
-        for h in (0, 1):
+        nc.vector.tensor_copy(scales_all[:, LEAD_BYTES:], scale_table[:].indirect(offsets[:]))
+        picked_scales = [scales_all[:, LEAD_BYTES : LEAD_BYTES + HALF], scales_all[:, LEAD_BYTES + HALF :]]
+        idle = psum.tile([N, S], F32, name="idle")
+        nc.tensor.matmul_mx(
+            out=idle[:],
+            lhsT=picked0[:, LEAD_WORDS : LEAD_WORDS + N].bitcast(FP8X4),
+            lhsT_scale=scales_all[:, LEAD_BYTES : LEAD_BYTES + N],
+            rhs=picked0[:, LEAD_WORDS:].bitcast(FP8X4),
+            rhs_scale=scales_all[:, LEAD_BYTES:],
+            start=True,
+            stop=True,
+        )
+
+        w1_grouped0 = interleave([w1_raw0], "w1_0")
+        w1_mx0 = quantize(w1_grouped0, "w1_0")
+        for h in range(4):
             product(w1_mx0, picked0[:, LEAD_WORDS + h * QUARTER : LEAD_WORDS + (h + 1) * QUARTER], picked_scales, 0, h, True, False)
-        nc.vector.tensor_copy(scales_second[:], scale_table[:].indirect(offsets[:, HALF // LIST_ROWS :]))
-        for h in (2, 3):
-            product(w1_mx0, picked0[:, LEAD_WORDS + h * QUARTER : LEAD_WORDS + (h + 1) * QUARTER], picked_scales, 0, h, True, False)
-        shifted_all = placed.tile([P, S], U8, name="shifted_all", align_bytes=64, offset=5 * RAW_BYTES + HALF)
-        shifted_scales = [shifted_all[:, :HALF], shifted_all[:, HALF:]]
+        w2_grouped0 = interleave([w2_raw0], "w2_0")
         shifted0 = placed.tile([P, S], I32, name="shifted0", align_bytes=64, offset=5 * RAW_BYTES + 4 * HALF)
         nc.vector.tensor_copy(shifted0[:], picked0[:, LEAD_WORDS - 1 : LEAD_WORDS - 1 + S])
-        nc.vector.tensor_copy(shifted_all[:, : HALF + 1], scales_first[:, LEAD_BYTES - 1 :])
-        nc.vector.tensor_copy(shifted_all[:, HALF + 1 :], scales_second[:, : HALF - 1])
-        w2_mx0 = quantize(w2_raw0, "w2_0")
+        shifted_all = placed.tile([P, S], U8, name="shifted_all", align_bytes=64, offset=5 * RAW_BYTES)
+        shifted_scales = [shifted_all[:, :HALF], shifted_all[:, HALF:]]
+        nc.vector.tensor_copy(shifted_all[:], scales_all[:, LEAD_BYTES - 1 : LEAD_BYTES - 1 + S])
+        w2_mx0 = quantize(w2_grouped0, "w2_0")
         for h, (first, width) in enumerate(pieces):
             product(w2_mx0, shifted0[:, first : first + width], shifted_scales, 0, h, False, False)
 
@@ -131,17 +148,17 @@ def tile_picked_listconv_relu_p_kernel(tc, x_words, x_scales, w1, w2, offs, out)
                 picked.bitcast(U32), table1[:].bitcast(U32).indirect(offsets[:, first // LIST_ROWS : (first + width) // LIST_ROWS])
             )
 
-        w1_mx1 = quantize(w1_raw1, "w1_1")
-        picked1 = keep.tile([P, S], I32, name="picked1", align_bytes=64)
+        w1_mx1 = quantize(interleave([w1_raw1], "w1_1"), "w1_1")
+        picked1 = placed.tile([P, S], I32, name="picked1", align_bytes=64, offset=RAW_BYTES)
         for first in (0, HALF):
             gather1(picked1[:, first : first + HALF], first, HALF)
         for h, (first, width) in enumerate(pieces):
             product(w1_mx1, picked1[:, first : first + width], picked_scales, 1, h, False, False)
         nc.vector.tensor_copy(shifted1_first[:, 1:], picked1[:, : HALF - 1])
-        w2_mx1 = quantize(w2_raw1, "w2_1")
+        w2_mx1 = quantize(interleave(w2_raw1, "w2_1"), "w2_1")
         for h in (0, 1):
             product(w2_mx1, shifted1_first[:, h * QUARTER : (h + 1) * QUARTER], shifted_scales, 1, h, False, True)
-        shifted1_second = placed.tile([P, HALF], I32, name="shifted1_second", align_bytes=64, offset=4 * RAW_BYTES)
+        shifted1_second = placed.tile([P, HALF], I32, name="shifted1_second", align_bytes=64, offset=4 * RAW_BYTES + RAW_BYTES // 2)
         nc.vector.tensor_copy(shifted1_second[:], picked1[:, HALF - 1 : S - 1])
         for h in (0, 1):
             product(w2_mx1, shifted1_second[:, h * QUARTER : (h + 1) * QUARTER], shifted_scales, 1, 2 + h, False, True)

@@ -118,17 +118,6 @@ def tile_picked_listconv_relu_p_kernel(tc, x_words, x_scales, w1, w2, offs, out)
         nc.vector.tensor_copy(picked0[:, LEAD_WORDS:].bitcast(U32), table0[:].bitcast(U32).indirect(offsets[:]))
         nc.vector.tensor_copy(scales_all[:, LEAD_BYTES:], scale_table[:].indirect(offsets[:]))
         picked_scales = [scales_all[:, LEAD_BYTES : LEAD_BYTES + HALF], scales_all[:, LEAD_BYTES + HALF :]]
-        idle = psum.tile([N, S], F32, name="idle")
-        nc.tensor.matmul_mx(
-            out=idle[:],
-            lhsT=picked0[:, LEAD_WORDS : LEAD_WORDS + N].bitcast(FP8X4),
-            lhsT_scale=scales_all[:, LEAD_BYTES : LEAD_BYTES + N],
-            rhs=picked0[:, LEAD_WORDS:].bitcast(FP8X4),
-            rhs_scale=scales_all[:, LEAD_BYTES:],
-            start=True,
-            stop=True,
-        )
-
         w1_grouped0 = interleave([w1_raw0], "w1_0")
         w1_mx0 = quantize(w1_grouped0, "w1_0")
         for h in range(4):

@@ -158,4 +158,4 @@ def tile_picked_listconv_relu_p_kernel(tc, x_words, x_scales, w1, w2, offs, out)
         nc.sync.dma_start(out=out[:, :HALF], in_=result[0][:])
         nc.scalar.activation(result[1][:, :QUARTER], acc[2][:], ACT.Relu)
         nc.vector.tensor_scalar_max(result[1][:, QUARTER:], acc[3][:], 0.0)
-        nc.scalar.dma_start(out=out[:, HALF:], in_=result[1][:])
+        nc.sync.dma_start(out=out[:, HALF:], in_=result[1][:])

@@ -152,10 +152,11 @@ def tile_picked_listconv_relu_p_kernel(tc, x_words, x_scales, w1, w2, offs, out)
         for h in (0, 1):
             product(w2_mx1, shifted1_second[:, h * QUARTER : (h + 1) * QUARTER], shifted_scales, 1, 2 + h, False, True)
 
-        result = [keep.tile([N, HALF], F32, name="result%d" % half) for half in range(2)]
-        nc.vector.tensor_scalar_max(result[0][:, :QUARTER], acc[0][:], 0.0)
-        nc.scalar.activation(result[0][:, QUARTER:], acc[1][:], ACT.Relu)
-        nc.sync.dma_start(out=out[:, :HALF], in_=result[0][:])
-        nc.scalar.activation(result[1][:, :QUARTER], acc[2][:], ACT.Relu)
-        nc.vector.tensor_scalar_max(result[1][:, QUARTER:], acc[3][:], 0.0)
-        nc.sync.dma_start(out=out[:, HALF:], in_=result[1][:])
+        first = keep.tile([N, QUARTER], F32, name="first")
+        rest = keep.tile([N, S - QUARTER], F32, name="rest")
+        nc.vector.tensor_scalar_max(first[:], acc[0][:], 0.0)
+        nc.sync.dma_start(out=out[:, :QUARTER], in_=first[:])
+        nc.scalar.activation(rest[:, :QUARTER], acc[1][:], ACT.Relu)
+        nc.scalar.activation(rest[:, QUARTER:HALF], acc[2][:], ACT.Relu)
+        nc.vector.tensor_scalar_max(rest[:, HALF:], acc[3][:], 0.0)
+        nc.sync.dma_start(out=out[:, QUARTER:], in_=rest[:])

@@ -154,9 +154,8 @@ def tile_picked_listconv_relu_p_kernel(tc, x_words, x_scales, w1, w2, offs, out)
 
         first = keep.tile([N, QUARTER], F32, name="first")
         rest = keep.tile([N, S - QUARTER], F32, name="rest")
-        nc.vector.tensor_scalar_max(first[:], acc[0][:], 0.0)
-        nc.sync.dma_start(out=out[:, :QUARTER], in_=first[:])
-        nc.scalar.activation(rest[:, :QUARTER], acc[1][:], ACT.Relu)
-        nc.scalar.activation(rest[:, QUARTER:HALF], acc[2][:], ACT.Relu)
-        nc.vector.tensor_scalar_max(rest[:, HALF:], acc[3][:], 0.0)
-        nc.sync.dma_start(out=out[:, QUARTER:], in_=rest[:])
+        nc.scalar.activation(first[:], acc[0][:], ACT.Relu)
+        nc.scalar.dma_start(out=out[:, :QUARTER], in_=first[:])
+        for h in (1, 2, 3):
+            nc.vector.tensor_scalar_max(rest[:, (h - 1) * QUARTER : h * QUARTER], acc[h][:], 0.0)
+        nc.scalar.dma_start(out=out[:, QUARTER:], in_=rest[:])

@@ -59,12 +59,10 @@ def tile_picked_listconv_relu_p_kernel(tc, x_words, x_scales, w1, w2, offs, out)
                 in_=x_scales[:, SCALE_ROWS * q : SCALE_ROWS * (q + 1), :].bitcast(I32),
             )
 
-        zero = placed.tile([P, 6 * RAW_BYTES // 4], I32, name="zero", align_bytes=64, offset=0)
-        nc.vector.memset(zero[:, :1], 0)
         scales_all = keep.tile([P, LEAD_BYTES + S], U8, name="scales_all", align_bytes=64)
         nc.vector.memset(scales_all[:, :LEAD_BYTES].bitcast(I32), 0)
         shifted1_first = keep.tile([P, HALF], I32, name="shifted1_first", align_bytes=64)
-        nc.vector.tensor_copy(shifted1_first[:, :1], zero[:, :1])
+        nc.vector.memset(shifted1_first[:, :1], 0)
         picked0 = keep.tile([P, LEAD_WORDS + S], I32, name="picked0", align_bytes=64)
         nc.vector.memset(picked0[:, :LEAD_WORDS], 0)
 

@@ -120,13 +120,13 @@ def tile_picked_listconv_relu_p_kernel(tc, x_words, x_scales, w1, w2, offs, out)
         w1_mx0 = quantize(w1_grouped0, "w1_0")
         for h in range(4):
             product(w1_mx0, picked0[:, LEAD_WORDS + h * QUARTER : LEAD_WORDS + (h + 1) * QUARTER], picked_scales, 0, h, True, False)
-        w2_grouped0 = interleave([w2_raw0], "w2_0")
-        shifted0 = placed.tile([P, S], I32, name="shifted0", align_bytes=64, offset=5 * RAW_BYTES + 4 * HALF)
+        shifted0 = placed.tile([P, S], I32, name="shifted0", align_bytes=64, offset=0)
         nc.vector.tensor_copy(shifted0[:], picked0[:, LEAD_WORDS - 1 : LEAD_WORDS - 1 + S])
+        w2_mx0 = quantize(interleave([w2_raw0], "w2_0"), "w2_0")
         shifted_all = placed.tile([P, S], U8, name="shifted_all", align_bytes=64, offset=5 * RAW_BYTES)
         shifted_scales = [shifted_all[:, :HALF], shifted_all[:, HALF:]]
-        nc.vector.tensor_copy(shifted_all[:], scales_all[:, LEAD_BYTES - 1 : LEAD_BYTES - 1 + S])
-        w2_mx0 = quantize(w2_grouped0, "w2_0")
+        for first in (0, HALF):
+            nc.vector.tensor_copy(shifted_all[:, first : first + HALF], scales_all[:, LEAD_BYTES - 1 + first : LEAD_BYTES - 1 + first + HALF])
         for h, (first, width) in enumerate(pieces):
             product(w2_mx0, shifted0[:, first : first + width], shifted_scales, 0, h, False, False)
 

@@ -27,6 +27,7 @@ LINE = 4
 HALF = S // 2
 FIRST_TOKENS = 256
 QUARTER = S // 4
+FIRST_STORE = 64
 RAW_BYTES = PACK * N * 4
 
 
@@ -150,10 +151,14 @@ def tile_picked_listconv_relu_p_kernel(tc, x_words, x_scales, w1, w2, offs, out)
         for h in (0, 1):
             product(w2_mx1, shifted1_second[:, h * QUARTER : (h + 1) * QUARTER], shifted_scales, 1, 2 + h, False, True)
 
-        first = keep.tile([N, QUARTER], F32, name="first")
-        rest = keep.tile([N, S - QUARTER], F32, name="rest")
-        nc.scalar.activation(first[:], acc[0][:], ACT.Relu)
-        nc.scalar.dma_start(out=out[:, :QUARTER], in_=first[:])
-        for h in (1, 2, 3):
-            nc.vector.tensor_scalar_max(rest[:, (h - 1) * QUARTER : h * QUARTER], acc[h][:], 0.0)
-        nc.scalar.dma_start(out=out[:, QUARTER:], in_=rest[:])
+        first = keep.tile([N, FIRST_STORE], F32, name="first")
+        second = keep.tile([N, HALF - FIRST_STORE], F32, name="second")
+        third = keep.tile([N, HALF], F32, name="third")
+        nc.scalar.activation(first[:], acc[0][:, :FIRST_STORE], ACT.Relu)
+        nc.scalar.dma_start(out=out[:, :FIRST_STORE], in_=first[:])
+        nc.scalar.activation(second[:, : QUARTER - FIRST_STORE], acc[0][:, FIRST_STORE:], ACT.Relu)
+        nc.vector.tensor_scalar_max(second[:, QUARTER - FIRST_STORE :], acc[1][:], 0.0)
+        nc.sync.dma_start(out=out[:, FIRST_STORE:HALF], in_=second[:])
+        nc.scalar.activation(third[:, :QUARTER], acc[2][:], ACT.Relu)
+        nc.vector.tensor_scalar_max(third[:, QUARTER:], acc[3][:], 0.0)
+        nc.scalar.dma_start(out=out[:, HALF:], in_=third[:])

from contextlib import ExitStack

import concourse.mybir as mybir

K, T, S, N = 1024, 1024, 512, 128
FLOPS = 2 * 2 * K * S * N

F32 = mybir.dt.float32
BF16 = mybir.dt.bfloat16
I32 = mybir.dt.int32
U32 = mybir.dt.uint32
U16 = mybir.dt.uint16
U8 = mybir.dt.uint8
FP8X4 = mybir.dt.float8_e4m3fn_x4
ACT = mybir.ActivationFunctionType

P = 128
PACK = 4
K_PASS = P * PACK
PASSES = K // K_PASS
QUADRANT = 32
SCALE_ROWS = 4
LIST_ROWS = 16
LEAD_WORDS = 16
LEAD_BYTES = 64
LINE = 4
HALF = S // 2
FIRST_TOKENS = 256
QUARTER = S // 4
FIRST_STORE = 64
RAW_BYTES = PACK * N * 4


def tile_picked_listconv_relu_p_kernel(tc, x_words, x_scales, w1, w2, offs, out):
    nc = tc.nc
    with ExitStack() as ctx:
        lists = ctx.enter_context(tc.tile_pool(name="lists", bufs=1))
        keep = ctx.enter_context(tc.tile_pool(name="keep", bufs=1))
        placed = ctx.enter_context(tc.tile_pool(name="placed", bufs=1))
        psum = ctx.enter_context(tc.psum_pool(name="psum", bufs=1))

        def load_words(table, g):
            nc.sync.dma_start(out=table[:], in_=x_words[g].rearrange("p c r -> p (c r)").bitcast(I32))

        def load_weights(raw, w, g):
            nc.sync.dma_start(out=raw[:], in_=w[g * K_PASS : (g + 1) * K_PASS, :].rearrange("(p t) n -> p t n", t=PACK))

        offsets = lists.tile([P, S // LIST_ROWS], U16, name="offsets")
        table0 = keep.tile([P, T], I32, name="table0", align_bytes=64)
        words0 = x_words[0].rearrange("p c r -> p (c r)").bitcast(I32)
        nc.sync.dma_start(out=table0[:, : FIRST_TOKENS], in_=words0[:, : FIRST_TOKENS])
        nc.sync.dma_start(offsets[:], offs)
        nc.sync.dma_start(out=table0[:, FIRST_TOKENS :], in_=words0[:, FIRST_TOKENS :])

        scale_table = keep.tile([P, T], U8, name="scale_table", align_bytes=64)
        nc.vector.memset(scale_table[:].bitcast(I32), 0)
        for q in range(P // QUADRANT):
            nc.sync.dma_start(
                out=scale_table[QUADRANT * q : QUADRANT * q + PASSES * SCALE_ROWS, :].bitcast(I32),
                in_=x_scales[:, SCALE_ROWS * q : SCALE_ROWS * (q + 1), :].bitcast(I32),
            )

        scales_all = keep.tile([P, LEAD_BYTES + S], U8, name="scales_all", align_bytes=64)
        nc.vector.memset(scales_all[:, :LEAD_BYTES].bitcast(I32), 0)
        shifted1_first = keep.tile([P, HALF], I32, name="shifted1_first", align_bytes=64)
        nc.vector.memset(shifted1_first[:, :1], 0)
        picked0 = keep.tile([P, LEAD_WORDS + S], I32, name="picked0", align_bytes=64)
        nc.vector.memset(picked0[:, :LEAD_WORDS], 0)

        w1_raw0 = placed.tile([P, PACK, N], F32, name="w1_raw0", align_bytes=64, offset=0)
        load_weights(w1_raw0, w1, 0)
        w2_raw0 = placed.tile([P, PACK, N], F32, name="w2_raw0", align_bytes=64, offset=5 * RAW_BYTES)
        load_weights(w2_raw0, w2, 0)
        w1_raw1 = placed.tile([P, PACK, N], F32, name="w1_raw1", align_bytes=64, offset=RAW_BYTES)
        load_weights(w1_raw1, w1, 1)
        table1 = placed.tile([P, T], I32, name="table1", align_bytes=64, offset=2 * RAW_BYTES)
        load_words(table1, 1)
        w2_rows1 = w2[K_PASS:, :].rearrange("(p t) n -> p t n", t=PACK)
        w2_raw1 = []
        for u in range(2):
            part = placed.tile([P, 2, N], F32, name="w2_raw1_%d" % u, align_bytes=64, offset=4 * RAW_BYTES + u * RAW_BYTES // 2)
            nc.sync.dma_start(out=part[:], in_=w2_rows1[:, 2 * u : 2 * u + 2, :])
            w2_raw1.append(part)

        pieces = [(first, QUARTER) for first in range(0, S, QUARTER)]
        acc = [psum.tile([N, width], F32, name="acc%d" % h) for h, (first, width) in enumerate(pieces)]

        def interleave(parts, label):
            grouped = keep.tile([P, N, PACK], BF16, name="grouped_" + label, tag="grouped_" + label, align_bytes=64)
            rows = PACK // len(parts)
            for u, raw in enumerate(parts):
                nc.scalar.activation(
                    grouped[:, :, rows * u : rows * (u + 1)].rearrange("p (c i) t -> p c t i", i=LINE),
                    raw[:].rearrange("p t (c i) -> p c t i", i=LINE),
                    ACT.Copy,
                )
            return grouped

        def quantize(grouped, label):
            codes = keep.tile([P, N], U32, name="codes_" + label, align_bytes=64)
            scales = keep.tile([P, N], U8, name="scales_" + label, align_bytes=64)
            nc.vector.quantize_mx(out=codes[:].bitcast(FP8X4), scales=scales[:], in_=grouped[:].rearrange("p n t -> p (n t)"))
            return codes, scales

        def product(weights, words, token_scales, g, h, start, stop):
            codes, scales = weights
            nc.tensor.matmul_mx(
                out=acc[h][:],
                lhsT=codes[:].bitcast(FP8X4),
                lhsT_scale=scales[:],
                rhs=words.bitcast(FP8X4),
                rhs_scale=token_scales[h // 2][SCALE_ROWS * g :, h % 2 * QUARTER : (h % 2 + 1) * QUARTER],
                start=start,
                stop=stop,
            )

        nc.vector.tensor_copy(picked0[:, LEAD_WORDS:].bitcast(U32), table0[:].bitcast(U32).indirect(offsets[:]))
        nc.vector.tensor_copy(scales_all[:, LEAD_BYTES:], scale_table[:].indirect(offsets[:]))
        picked_scales = [scales_all[:, LEAD_BYTES : LEAD_BYTES + HALF], scales_all[:, LEAD_BYTES + HALF :]]
        w1_grouped0 = interleave([w1_raw0], "w1_0")
        w1_mx0 = quantize(w1_grouped0, "w1_0")
        for h in range(4):
            product(w1_mx0, picked0[:, LEAD_WORDS + h * QUARTER : LEAD_WORDS + (h + 1) * QUARTER], picked_scales, 0, h, True, False)
        shifted0 = placed.tile([P, S], I32, name="shifted0", align_bytes=64, offset=0)
        nc.vector.tensor_copy(shifted0[:], picked0[:, LEAD_WORDS - 1 : LEAD_WORDS - 1 + S])
        w2_mx0 = quantize(interleave([w2_raw0], "w2_0"), "w2_0")
        shifted_all = placed.tile([P, S], U8, name="shifted_all", align_bytes=64, offset=5 * RAW_BYTES)
        shifted_scales = [shifted_all[:, :HALF], shifted_all[:, HALF:]]
        for first in (0, HALF):
            nc.vector.tensor_copy(shifted_all[:, first : first + HALF], scales_all[:, LEAD_BYTES - 1 + first : LEAD_BYTES - 1 + first + HALF])
        for h, (first, width) in enumerate(pieces):
            product(w2_mx0, shifted0[:, first : first + width], shifted_scales, 0, h, False, False)

        def gather1(picked, first, width):
            nc.vector.tensor_copy(
                picked.bitcast(U32), table1[:].bitcast(U32).indirect(offsets[:, first // LIST_ROWS : (first + width) // LIST_ROWS])
            )

        w1_mx1 = quantize(interleave([w1_raw1], "w1_1"), "w1_1")
        picked1 = placed.tile([P, S], I32, name="picked1", align_bytes=64, offset=RAW_BYTES)
        for first in (0, HALF):
            gather1(picked1[:, first : first + HALF], first, HALF)
        for h, (first, width) in enumerate(pieces):
            product(w1_mx1, picked1[:, first : first + width], picked_scales, 1, h, False, False)
        nc.vector.tensor_copy(shifted1_first[:, 1:], picked1[:, : HALF - 1])
        w2_mx1 = quantize(interleave(w2_raw1, "w2_1"), "w2_1")
        for h in (0, 1):
            product(w2_mx1, shifted1_first[:, h * QUARTER : (h + 1) * QUARTER], shifted_scales, 1, h, False, True)
        shifted1_second = placed.tile([P, HALF], I32, name="shifted1_second", align_bytes=64, offset=4 * RAW_BYTES + RAW_BYTES // 2)
        nc.vector.tensor_copy(shifted1_second[:], picked1[:, HALF - 1 : S - 1])
        for h in (0, 1):
            product(w2_mx1, shifted1_second[:, h * QUARTER : (h + 1) * QUARTER], shifted_scales, 1, 2 + h, False, True)

        first = keep.tile([N, FIRST_STORE], F32, name="first")
        second = keep.tile([N, HALF - FIRST_STORE], F32, name="second")
        third = keep.tile([N, HALF], F32, name="third")
        nc.scalar.activation(first[:], acc[0][:, :FIRST_STORE], ACT.Relu)
        nc.scalar.dma_start(out=out[:, :FIRST_STORE], in_=first[:])
        nc.scalar.activation(second[:, : QUARTER - FIRST_STORE], acc[0][:, FIRST_STORE:], ACT.Relu)
        nc.vector.tensor_scalar_max(second[:, QUARTER - FIRST_STORE :], acc[1][:], 0.0)
        nc.sync.dma_start(out=out[:, FIRST_STORE:HALF], in_=second[:])
        nc.scalar.activation(third[:, :QUARTER], acc[2][:], ACT.Relu)
        nc.vector.tensor_scalar_max(third[:, QUARTER:], acc[3][:], 0.0)
        nc.scalar.dma_start(out=out[:, HALF:], in_=third[:])
